import numpy as np
import ml_dtypes


def mxq(x, axis, fmt="e4m3"):
    dtype, down = {"e4m3": (ml_dtypes.float8_e4m3fn, 7), "e5m2": (ml_dtypes.float8_e5m2, 14)}[fmt]
    v = np.moveaxis(np.asarray(x, np.float32).astype(ml_dtypes.bfloat16).astype(np.float64), axis, -1)
    blocks = v.reshape(v.shape[:-1] + (-1, 32))
    amax = np.abs(blocks).max(-1, keepdims=True)
    byte = np.maximum(np.where(amax > 0, np.frexp(amax)[1] - 1 + 127, 0) - down, 1)
    scale = np.exp2(byte - 127.0)
    codes = (blocks / scale).astype(np.float32).astype(dtype).astype(np.float64)
    return np.moveaxis((codes * scale).reshape(v.shape), -1, axis)


WIDE = False


def mx_kscale(k):
    if not WIDE:
        return np.ones(k)
    levels = np.array([10, -10, 5, -5, 0])
    if k % 512:
        return np.exp2(np.random.permutation(np.resize(levels, k // 32))).repeat(32)
    a = np.empty((k // 512, 16))
    for p in range(k // 512):
        a[p, :8] = np.random.permutation(np.resize(levels, 8))
        for g in range(8):
            far = levels[np.abs(levels - a[p, g]) >= 10]
            a[p, g + 8] = far[np.random.randint(len(far))]
    return np.exp2(a.ravel()).repeat(32)


def f64(x):
    return np.asarray(x).astype(np.float64)


def striped(idx):
    return np.tile(idx.reshape(-1, 16).T, (8, 1)).astype(np.uint16)


def unstriped(offs):
    return offs[:16].T.reshape(-1).astype(np.int64)


E2M1 = np.array([0.0, 0.5, 1.0, 1.5, 2.0, 3.0, 4.0, 6.0, -0.0, -0.5, -1.0, -1.5, -2.0, -3.0, -4.0, -6.0])


def pack_weight(w, fmt):
    k, n = w.shape
    w = f64(np.asarray(w, np.float32).astype(ml_dtypes.bfloat16)).reshape(k // 32, 32, n)
    amax = np.abs(w).max(1)
    if fmt == "e4m3":
        byte = np.frexp(amax)[1] - 1 + 127 - 7
    else:
        mant, ex = np.frexp(amax / 6.0)
        byte = np.where(mant > 0.5, ex, ex - 1) + 127
    byte = np.clip(np.where(amax > 0, byte, 1), 1, 254)
    scaled = (w * np.exp2(127.0 - byte)[:, None, :]).reshape(k, n).astype(np.float32)
    by_word = np.ascontiguousarray(scaled.reshape(k // 512, 128, 4, n).transpose(0, 1, 3, 2))
    if fmt == "e4m3":
        words = by_word.astype(ml_dtypes.float8_e4m3fn).view(np.uint8)
    else:
        c = by_word.astype(ml_dtypes.float4_e2m1fn).view(np.uint8) & 0xF
        words = (c[..., 0::2] | (c[..., 1::2] << 4)).reshape(k // 512, 128, 2 * n)
    return np.ascontiguousarray(words), np.ascontiguousarray(byte.astype(np.uint8).reshape(k // 512, 16, n))


def unpack_weight(words, scales, fmt):
    g, _, n = scales.shape
    words = np.ascontiguousarray(words).reshape(g, 128, n, -1)
    if fmt == "e4m3":
        vals = words.view(ml_dtypes.float8_e4m3fn).astype(np.float64)
    else:
        nib = np.empty((g, 128, n, 4), np.uint8)
        nib[..., 0::2] = words & 0xF
        nib[..., 1::2] = words >> 4
        vals = E2M1[nib]
    vals = vals * np.repeat(np.exp2(scales.astype(np.float64) - 127.0), 8, axis=1)[..., None]
    return vals.transpose(0, 1, 3, 2).reshape(g * 512, n)


def gelu(v):
    return 0.5 * v * (1.0 + np.tanh(np.sqrt(2.0 / np.pi) * (v + 0.044715 * v**3)))


K, T, S, H, T2, N, P = 1024, 4096, 1024, 1024, 2048, 512, 128

def setup_inputs():
    n = np.random.standard_normal
    s = mx_kscale(K)[:, None]
    u = mx_kscale(H)[:, None]
    tab_words, tab_scales = pack_weight(n((K, T)) * s, "e4m3")
    w2_words, w2_scales = pack_weight(n((H, N)) / np.sqrt(H) / u, "e2m1")
    return {
        "tab_words": tab_words, "tab_scales": tab_scales,
        "offs": striped(np.random.permutation(T)[:S]),
        "w1": (n((K, H)) / np.sqrt(K) / s * u.T).astype(np.float32),
        "b1": (0.5 * n(H) * u[:, 0]).astype(np.float32),
        "wgs": np.exp(0.3 * n((P, S))).astype(np.float32),
        "offs2": striped(np.random.permutation(T2)[:S]),
        "old": (n((H, T2)) * u).astype(np.float32),
        "w2_words": w2_words, "w2_scales": w2_scales,
        "bo": (0.5 * n(N)).astype(np.float32),
    }

def reference(tab_words, tab_scales, offs, w1, b1, wgs, offs2, old, w2_words, w2_scales, bo):
    v = unpack_weight(tab_words, tab_scales, "e4m3")[:, unstriped(offs)]
    w1q = mxq(f64(w1), 0, "e4m3")
    h = np.maximum((w1q.T @ v) + f64(b1)[:, None], 0.0)
    page = np.zeros((H, T2))
    page[:, unstriped(offs2)] = np.tile(f64(wgs), (H // P, 1)) * h
    z = page + f64(old)
    zq = mxq(z, 0, "e4m3")
    w2 = unpack_weight(w2_words, w2_scales, "e2m1")
    return (w2.T @ zq) + f64(bo)[:, None]

@@ -1,0 +1,322 @@
+from contextlib import ExitStack
+
+import concourse.mybir as mybir
+from concourse.masks import make_identity
+
+K, T, S, H, T2, N = 1024, 4096, 1024, 1024, 2048, 512
+FLOPS = 2 * K * H * S + 2 * H * N * T2
+
+F32 = mybir.dt.float32
+BF16 = mybir.dt.bfloat16
+I32 = mybir.dt.int32
+U32 = mybir.dt.uint32
+U16 = mybir.dt.uint16
+U8 = mybir.dt.uint8
+FP8X4 = mybir.dt.float8_e4m3fn_x4
+FP4X4 = mybir.dt.float4_e2m1fn_x4
+ACT = mybir.ActivationFunctionType
+ALU = mybir.AluOpType
+
+P = 128
+BANK = 512
+PASSES = 2
+SLICES = H // P
+CHUNKS = T2 // BANK
+N_TILES = N // P
+HALVES = S // BANK
+W1_LOADS = (1, 1, 2, 2, 2)
+PAGE_BUFS = 3
+OLD_BUFS = 4
+H_BUFS = 3
+CAST_BUFS = 3
+WOVEN_BUFS = 3
+PARKED = (4, 3, 3, 2)
+
+
+def tile_list_paged_cache_write_kernel(
+    tc, tab_words, tab_scales, offs, w1, b1, wgs, offs2, old, w2_words, w2_scales, bo, out
+):
+    nc = tc.nc
+    with ExitStack() as ctx:
+        keep = ctx.enter_context(tc.tile_pool(name="keep", bufs=1))
+        wide = ctx.enter_context(tc.tile_pool(name="wide", bufs=2))
+        psum = ctx.enter_context(tc.psum_pool(name="psum", bufs=1))
+
+        banks = [psum.tile([P, BANK], F32, name="bank%d" % i) for i in range(8)]
+        h_banks = banks[0:2]
+        sum_banks = [banks[2], banks[3], banks[6], banks[7]]
+        word_banks = banks[4:6]
+        out_banks = h_banks + sum_banks
+
+        def tiles(name, count, shape, dtype):
+            return [keep.tile(shape, dtype, name="%s%d" % (name, i), align_bytes=64) for i in range(count)]
+
+        list1 = keep.tile([P, S // 16], U16, name="list1")
+        list2 = keep.tile([P, S // 16], U16, name="list2")
+        table = [wide.tile([P, T], U32, name="table%d" % a, tag="wide", align_bytes=64) for a in range(PASSES)]
+        table_scales = keep.tile([P, T], U8, name="table_scales", align_bytes=64)
+        v_first = keep.tile([P, S], U32, name="v_first", align_bytes=64)
+        v_second = tiles("v_second", HALVES, [P, BANK], U32)
+        v_scales = keep.tile([P, S], U8, name="v_scales", align_bytes=64)
+        w1_raw = [
+            keep.tile([P, PASSES, 4, n * P], F32, name="w1_raw%d" % i, align_bytes=64) for i, n in enumerate(W1_LOADS)
+        ]
+        w1_cast = tiles("w1_cast", CAST_BUFS, [P, PASSES * P * 4], BF16)
+        w1_words = tiles("w1_words", SLICES, [P, PASSES * P], U32)
+        w1_scales = tiles("w1_scales", SLICES, [P, PASSES * P], U8)
+        wgs_sb = keep.tile([P, S], F32, name="wgs_sb")
+        old_sb = tiles("old_sb", OLD_BUFS, [P, T2], F32)
+        pages = tiles("page", PAGE_BUFS, [P, T2], F32)
+        h_sb = tiles("h_sb", H_BUFS, [P, S], F32)
+        z_turned = tiles("z_turned", CHUNKS + 1, [P, 4, 2, 2 * P], BF16)
+        z_woven = tiles("z_woven", WOVEN_BUFS, [P, BANK * 4], BF16)
+        z_words = tiles("z_words", PASSES * CHUNKS, [P, BANK], U32)
+        z_scales = tiles("z_scales", PASSES * CHUNKS, [P, BANK], U8)
+        w2_sb = keep.tile([P, PASSES, 2 * N], U8, name="w2_sb", align_bytes=64)
+        w2_planes = keep.tile([P, PASSES, N], U8, name="w2_planes", align_bytes=64)
+        ident = keep.tile([P, P], F32, name="ident")
+        bias_rows = keep.tile([P, P], F32, name="bias_rows")
+        bias = keep.tile([P, SLICES + N_TILES], F32, name="bias")
+
+        w1_place = []
+        for i, n in enumerate(W1_LOADS):
+            w1_place.extend([(i, j) for j in range(n)])
+
+        def load_w1(i):
+            first = sum(W1_LOADS[:i]) * P
+            cols = slice(first, first + W1_LOADS[i] * P)
+            for a in range(PASSES):
+                rows = w1[a * BANK : (a + 1) * BANK, cols]
+                nc.sync.dma_start(out=w1_raw[i][:, a], in_=rows.rearrange("(p j) c -> p j c", j=4))
+
+        def load_table(a):
+            nc.sync.dma_start(
+                out=table[a][:].bitcast(I32), in_=tab_words[a].rearrange("p t i -> p (t i)").bitcast(I32)
+            )
+
+        def load_old(s):
+            nc.sync.dma_start(out=old_sb[s % OLD_BUFS][:], in_=old[s * P : (s + 1) * P, :])
+
+        def cast_w1(s, copy):
+            i, j = w1_place[s]
+            raw = w1_raw[i][:, :, :, j * P : (j + 1) * P]
+            copy(
+                out=w1_cast[s % CAST_BUFS][:].rearrange("p (a c i j) -> p a c j i", a=PASSES, i=4, j=4),
+                in_=raw.rearrange("p a j (c i) -> p a c j i", i=4),
+            )
+
+        def quantize_w1(s):
+            nc.vector.quantize_mx(
+                out=w1_words[s][:].bitcast(FP8X4), scales=w1_scales[s][:], in_=w1_cast[s % CAST_BUFS][:]
+            )
+
+        def entries(lst, half):
+            return lst[:, half * (BANK // 16) : (half + 1) * (BANK // 16)]
+
+        def v_words(a, half):
+            return v_first[:, half * BANK : (half + 1) * BANK] if a == 0 else v_second[half][:]
+
+        def first_layer(s, into):
+            for half in range(HALVES):
+                for a in range(PASSES):
+                    cols = slice(a * P, (a + 1) * P)
+                    nc.tensor.matmul_mx(
+                        out=into[half][:],
+                        lhsT=w1_words[s][:, cols].bitcast(FP8X4),
+                        lhsT_scale=w1_scales[s][:, cols],
+                        rhs=v_words(a, half).bitcast(FP8X4),
+                        rhs_scale=v_scales[4 * a : P, half * BANK : (half + 1) * BANK],
+                        start=(a == 0),
+                        stop=(a == PASSES - 1),
+                    )
+                nc.scalar.activation(
+                    out=h_sb[s % H_BUFS][:, half * BANK : (half + 1) * BANK],
+                    in_=into[half][:],
+                    func=ACT.Relu,
+                    bias=bias[:, s : s + 1],
+                )
+
+        def scatter(s):
+            page, h = pages[s % PAGE_BUFS], h_sb[s % H_BUFS]
+            if s == 0:
+                for half in range(HALVES):
+                    cols = slice(half * BANK, (half + 1) * BANK)
+                    nc.vector.tensor_tensor(
+                        page[:].indirect(entries(list2, half)), h[:, cols], wgs_sb[:, cols], ALU.mult
+                    )
+            else:
+                nc.vector.tensor_tensor(page[:].indirect(list2[:]), h[:], wgs_sb[:], ALU.mult)
+
+        def turn(src, c, start, stop):
+            for q in range(4):
+                cols = slice(c * BANK + q * P, c * BANK + (q + 1) * P)
+                nc.tensor.matmul(
+                    sum_banks[c][:, q * P : (q + 1) * P],
+                    lhsT=src[:, cols],
+                    rhs=ident[:],
+                    is_transpose=True,
+                    start=(start and q == 0),
+                    stop=(stop and q == 3),
+                )
+
+        def turned(a, c):
+            return z_turned[(a * CHUNKS + c) % len(z_turned)]
+
+        def round_sum(s, c, copy):
+            a, sq = divmod(s, 4)
+            copy(
+                out=turned(a, c)[:, :, :, sq * 64 : (sq + 1) * 64].rearrange("p q u (m e) -> p u q m e", e=2),
+                in_=sum_banks[c][:].rearrange("p (q m u e) -> p u q m e", q=4, u=2, e=2),
+            )
+
+        def turn_back(a, c, copies):
+            words = turned(a, c)[:].rearrange("p q u w -> p (q u w)").bitcast(F32)
+            woven = z_woven[(a * CHUNKS + c) % WOVEN_BUFS][:].bitcast(F32)
+            for b in range(2):
+                for i in range(4):
+                    nc.tensor.transpose(
+                        word_banks[b][:, i * P : (i + 1) * P],
+                        words[:, (4 * b + i) * P : (4 * b + i + 1) * P],
+                        ident[:],
+                    )
+                copies[b](
+                    out=woven[:, b * BANK : (b + 1) * BANK].rearrange("p (q t u) -> p q t u", q=2, u=2),
+                    in_=word_banks[b][:].rearrange("p (q u t) -> p q t u", q=2, u=2),
+                )
+
+        def quantize_z(a, c):
+            i = a * CHUNKS + c
+            nc.vector.quantize_mx(out=z_words[i][:].bitcast(FP8X4), scales=z_scales[i][:], in_=z_woven[i % WOVEN_BUFS][:])
+
+        def second_layer(bank, c, n, a, start, stop):
+            nc.tensor.matmul_mx(
+                out=bank[:],
+                lhsT=w2_sb[:, a, 2 * n * P : 2 * (n + 1) * P].bitcast(FP4X4),
+                lhsT_scale=w2_planes[:, a, n * P : (n + 1) * P],
+                rhs=z_words[a * CHUNKS + c][:].bitcast(FP8X4),
+                rhs_scale=z_scales[a * CHUNKS + c][:],
+                start=start,
+                stop=stop,
+            )
+
+        nc.vector.memset(bias_rows[:], 0.0)
+        nc.vector.memset(table_scales[:].bitcast(I32), 0)
+        make_identity(nc, ident[:])
+        for q in range(4):
+            nc.gpsimd.dma_start(
+                out=table_scales[32 * q : 32 * q + 8, :].bitcast(I32),
+                in_=tab_scales[:, 4 * q : 4 * q + 4, :].bitcast(I32),
+            )
+        for page in pages:
+            nc.vector.memset(page[:], 0.0)
+        nc.vector.memset(w2_planes[:].rearrange("p a c -> p (a c)").bitcast(I32), 0)
+
+        nc.scalar.dma_start(out=bias_rows[0:SLICES, :], in_=b1.rearrange("(s p) -> s p", p=P))
+        nc.scalar.dma_start(out=bias_rows[SLICES : SLICES + N_TILES, :], in_=bo.rearrange("(s p) -> s p", p=P))
+        nc.sync.dma_start(list1[:], offs)
+        load_table(0)
+        load_w1(0)
+        load_table(1)
+        nc.sync.dma_start(list2[:], offs2)
+        nc.sync.dma_start(out=wgs_sb[:], in_=wgs)
+        load_w1(1)
+        load_w1(2)
+        load_old(0)
+        load_old(1)
+        load_w1(3)
+        load_old(2)
+        load_w1(4)
+        load_old(3)
+        nc.sync.dma_start(out=w2_sb[:].bitcast(I32), in_=w2_words.rearrange("a p c -> p a c").bitcast(I32))
+        for q in range(4):
+            nc.sync.dma_start(
+                out=w2_planes[32 * q : 32 * q + 4].bitcast(I32),
+                in_=w2_scales[:, 4 * q : 4 * q + 4, :].rearrange("a r c -> r a c").bitcast(I32),
+            )
+
+        nc.tensor.transpose(word_banks[0][:, 0:P], bias_rows[:], ident[:])
+        nc.scalar.activation(out=bias[:], in_=word_banks[0][:, 0 : SLICES + N_TILES], func=ACT.Identity)
+
+        nc.vector.tensor_copy(v_first[:], table[0][:].indirect(list1[:]))
+        nc.vector.tensor_copy(v_scales[:], table_scales[:].indirect(list1[:]))
+        cast_w1(0, nc.scalar.copy)
+        quantize_w1(0)
+        for half in range(HALVES):
+            nc.vector.tensor_copy(v_second[half][:], table[1][:].indirect(entries(list1, half)))
+        first_layer(0, h_banks)
+        cast_w1(1, nc.scalar.copy)
+        quantize_w1(1)
+        first_layer(1, h_banks)
+        cast_w1(2, nc.scalar.copy)
+
+        staged = [wide.tile([P, 2, N_TILES, BANK], F32, name="staged%d" % i, tag="wide", align_bytes=64) for i in range(2)]
+
+        def staging(c, n):
+            return staged[c // 2][:, c % 2, n, :]
+
+        def out_bias(n):
+            return bias[:, SLICES + n : SLICES + n + 1]
+
+        held = [(0, 0), (0, 1)]
+        parked = [(c, n) for c in range(CHUNKS) for n in range(N_TILES) if n < PARKED[c] and (c, n) not in held]
+        spare_banks = word_banks + h_banks
+
+        def park(i):
+            c, n = parked[i]
+            bank = spare_banks[i % len(spare_banks)]
+            second_layer(bank, c, n, 0, True, True)
+            nc.scalar.activation(out=staging(c, n), in_=bank[:], func=ACT.Identity, bias=out_bias(n))
+
+        for s in range(SLICES):
+            if s + 2 < SLICES:
+                quantize_w1(s + 2)
+            scatter(s)
+            if s == 4:
+                for c in range(CHUNKS):
+                    turn_back(0, c, (nc.scalar.copy, nc.scalar.copy))
+                    quantize_z(0, c)
+            if s + 2 < SLICES:
+                first_layer(s + 2, word_banks if s == 4 else h_banks)
+            if s + 3 < SLICES:
+                cast_w1(s + 3, nc.scalar.copy)
+            for c in range(CHUNKS):
+                turn(old_sb[s % OLD_BUFS], c, True, False)
+            if s + OLD_BUFS < SLICES:
+                load_old(s + OLD_BUFS)
+            if s == SLICES - 2:
+                for i in range(len(parked) // 2):
+                    park(i)
+            if s == SLICES - 1:
+                for i in range(len(parked) // 2, len(parked)):
+                    park(i)
+                for c, n in held:
+                    second_layer(h_banks[n], c, n, 0, True, False)
+            for c in range(CHUNKS):
+                turn(pages[s % PAGE_BUFS], c, False, True)
+            if s < SLICES - 1:
+                for c in range(CHUNKS):
+                    round_sum(s, c, nc.scalar.copy)
+
+        for c in range(CHUNKS):
+            round_sum(SLICES - 1, c, nc.scalar.copy if c % 2 == 0 else nc.vector.tensor_copy)
+
+        def finish(c):
+            for n in range(N_TILES):
+                bank = out_banks[(c * N_TILES + n) % len(out_banks)]
+                dst = staging(c, n)
+                if (c, n) in parked:
+                    second_layer(bank, c, n, 1, True, True)
+                    nc.vector.tensor_tensor(dst, bank[:], dst, ALU.add)
+                else:
+                    if (c, n) not in held:
+                        second_layer(bank, c, n, 0, True, False)
+                    second_layer(bank, c, n, 1, False, True)
+                    nc.scalar.activation(out=dst, in_=bank[:], func=ACT.Identity, bias=out_bias(n))
+                nc.sync.dma_start(out=out[n * P : (n + 1) * P, c * BANK : (c + 1) * BANK], in_=dst)
+
+        for c in range(CHUNKS):
+            turn_back(1, c, (nc.scalar.copy, nc.scalar.copy))
+            quantize_z(1, c)
+            if c > 0:
+                finish(c - 1)
+        finish(CHUNKS - 1)

@@ -25,12 +25,10 @@ CHUNKS = T2 // BANK
 N_TILES = N // P
 HALVES = S // BANK
 W1_LOADS = (1, 1, 2, 2, 2)
-PAGE_BUFS = 3
+PAGE_BUFS = 2
 OLD_BUFS = 4
 H_BUFS = 3
-CAST_BUFS = 3
-WOVEN_BUFS = 3
-PARKED = (4, 3, 3, 2)
+WOVEN_BUFS = 5
 
 
 def tile_list_paged_cache_write_kernel(
@@ -40,6 +38,7 @@ def tile_list_paged_cache_write_kernel(
     with ExitStack() as ctx:
         keep = ctx.enter_context(tc.tile_pool(name="keep", bufs=1))
         wide = ctx.enter_context(tc.tile_pool(name="wide", bufs=2))
+        reuse = ctx.enter_context(tc.tile_pool(name="reuse", bufs=1))
         psum = ctx.enter_context(tc.psum_pool(name="psum", bufs=1))
 
         banks = [psum.tile([P, BANK], F32, name="bank%d" % i) for i in range(8)]
@@ -54,21 +53,28 @@ def tile_list_paged_cache_write_kernel(
         list1 = keep.tile([P, S // 16], U16, name="list1")
         list2 = keep.tile([P, S // 16], U16, name="list2")
         table = [wide.tile([P, T], U32, name="table%d" % a, tag="wide", align_bytes=64) for a in range(PASSES)]
-        table_scales = keep.tile([P, T], U8, name="table_scales", align_bytes=64)
+        table_scales = reuse.tile([P, T], U8, name="table_scales", align_bytes=64, offset=1024)
         v_first = keep.tile([P, S], U32, name="v_first", align_bytes=64)
-        v_second = tiles("v_second", HALVES, [P, BANK], U32)
+        v_second = reuse.tile([P, S], U32, name="v_second", align_bytes=64, offset=2048)
         v_scales = keep.tile([P, S], U8, name="v_scales", align_bytes=64)
         w1_raw = [
-            keep.tile([P, PASSES, 4, n * P], F32, name="w1_raw%d" % i, align_bytes=64) for i, n in enumerate(W1_LOADS)
+            keep.tile([P, PASSES, 4, n * P], F32, name="w1_raw%d" % i, align_bytes=64)
+            if i != 1
+            else reuse.tile([P, PASSES, 4, n * P], F32, name="w1_raw1", align_bytes=64, offset=6144)
+            for i, n in enumerate(W1_LOADS)
         ]
-        w1_cast = tiles("w1_cast", CAST_BUFS, [P, PASSES * P * 4], BF16)
-        w1_words = tiles("w1_words", SLICES, [P, PASSES * P], U32)
+        cast_third = reuse.tile([P, PASSES * P * 4], BF16, name="cast_third", align_bytes=64, offset=8192)
+        h_late = reuse.tile([P, BANK], F32, name="h_late", align_bytes=64, offset=6144)
+        cast_first = keep.tile([P, PASSES * P * 4], BF16, name="cast_first", align_bytes=64)
+        cast_later = reuse.tile([P, PASSES * P * 4], BF16, name="cast_later", align_bytes=64, offset=0)
+        w1_words = [reuse.tile([P, PASSES * P], U32, name="w1_words_first", align_bytes=64, offset=1024)]
+        w1_words.extend(tiles("w1_words", SLICES - 1, [P, PASSES * P], U32))
         w1_scales = tiles("w1_scales", SLICES, [P, PASSES * P], U8)
         wgs_sb = keep.tile([P, S], F32, name="wgs_sb")
         old_sb = tiles("old_sb", OLD_BUFS, [P, T2], F32)
-        pages = tiles("page", PAGE_BUFS, [P, T2], F32)
+        pages = tiles("page", PAGE_BUFS, [P, T2 + 1], F32)
         h_sb = tiles("h_sb", H_BUFS, [P, S], F32)
-        z_turned = tiles("z_turned", CHUNKS + 1, [P, 4, 2, 2 * P], BF16)
+        z_turned = tiles("z_turned", PASSES * CHUNKS, [P, 4, 2, 2 * P], BF16)
         z_woven = tiles("z_woven", WOVEN_BUFS, [P, BANK * 4], BF16)
         z_words = tiles("z_words", PASSES * CHUNKS, [P, BANK], U32)
         z_scales = tiles("z_scales", PASSES * CHUNKS, [P, BANK], U8)
@@ -97,31 +103,39 @@ def tile_list_paged_cache_write_kernel(
         def load_old(s):
             nc.sync.dma_start(out=old_sb[s % OLD_BUFS][:], in_=old[s * P : (s + 1) * P, :])
 
-        def cast_w1(s, copy):
+        def w1_cast(s):
+            return {0: cast_first, 2: cast_third}.get(s, cast_later)
+
+        def cast_w1(s):
             i, j = w1_place[s]
             raw = w1_raw[i][:, :, :, j * P : (j + 1) * P]
-            copy(
-                out=w1_cast[s % CAST_BUFS][:].rearrange("p (a c i j) -> p a c j i", a=PASSES, i=4, j=4),
-                in_=raw.rearrange("p a j (c i) -> p a c j i", i=4),
+            nc.scalar.copy(
+                out=w1_cast(s)[:].rearrange("p (a c j) -> p a c j", a=PASSES, j=4),
+                in_=raw.rearrange("p a j c -> p a c j"),
             )
 
         def quantize_w1(s):
             nc.vector.quantize_mx(
-                out=w1_words[s][:].bitcast(FP8X4), scales=w1_scales[s][:], in_=w1_cast[s % CAST_BUFS][:]
+                out=w1_words[s][:].bitcast(FP8X4), scales=w1_scales[s][:], in_=w1_cast(s)[:]
             )
 
         def entries(lst, half):
             return lst[:, half * (BANK // 16) : (half + 1) * (BANK // 16)]
 
         def v_words(a, half):
-            return v_first[:, half * BANK : (half + 1) * BANK] if a == 0 else v_second[half][:]
+            return (v_first if a == 0 else v_second)[:, half * BANK : (half + 1) * BANK]
 
-        def first_layer(s, into):
+        def h_half(s, half):
+            if s == 0 and half == 1:
+                return h_late[:]
+            return h_sb[s % H_BUFS][:, half * BANK : (half + 1) * BANK]
+
+        def first_layer(s):
             for half in range(HALVES):
                 for a in range(PASSES):
                     cols = slice(a * P, (a + 1) * P)
                     nc.tensor.matmul_mx(
-                        out=into[half][:],
+                        out=h_banks[half][:],
                         lhsT=w1_words[s][:, cols].bitcast(FP8X4),
                         lhsT_scale=w1_scales[s][:, cols],
                         rhs=v_words(a, half).bitcast(FP8X4),
@@ -129,9 +143,11 @@ def tile_list_paged_cache_write_kernel(
                         start=(a == 0),
                         stop=(a == PASSES - 1),
                     )
+                if s == 0 and half == 1:
+                    cast_w1(1)
                 nc.scalar.activation(
-                    out=h_sb[s % H_BUFS][:, half * BANK : (half + 1) * BANK],
-                    in_=into[half][:],
+                    out=h_half(s, half),
+                    in_=h_banks[half][:],
                     func=ACT.Relu,
                     bias=bias[:, s : s + 1],
                 )
@@ -142,7 +158,7 @@ def tile_list_paged_cache_write_kernel(
                 for half in range(HALVES):
                     cols = slice(half * BANK, (half + 1) * BANK)
                     nc.vector.tensor_tensor(
-                        page[:].indirect(entries(list2, half)), h[:, cols], wgs_sb[:, cols], ALU.mult
+                        page[:].indirect(entries(list2, half)), h_half(s, half), wgs_sb[:, cols], ALU.mult
                     )
             else:
                 nc.vector.tensor_tensor(page[:].indirect(list2[:]), h[:], wgs_sb[:], ALU.mult)
@@ -160,7 +176,7 @@ def tile_list_paged_cache_write_kernel(
                 )
 
         def turned(a, c):
-            return z_turned[(a * CHUNKS + c) % len(z_turned)]
+            return z_turned[a * CHUNKS + c]
 
         def round_sum(s, c, copy):
             a, sq = divmod(s, 4)
@@ -199,8 +215,8 @@ def tile_list_paged_cache_write_kernel(
                 stop=stop,
             )
 
-        nc.vector.memset(bias_rows[:], 0.0)
         nc.vector.memset(table_scales[:].bitcast(I32), 0)
+        nc.vector.memset(bias_rows[:], 0.0)
         make_identity(nc, ident[:])
         for q in range(4):
             nc.gpsimd.dma_start(
@@ -218,8 +234,9 @@ def tile_list_paged_cache_write_kernel(
         load_w1(0)
         load_table(1)
         nc.sync.dma_start(list2[:], offs2)
-        nc.sync.dma_start(out=wgs_sb[:], in_=wgs)
+        nc.sync.dma_start(out=wgs_sb[:, 0:BANK], in_=wgs[:, 0:BANK])
         load_w1(1)
+        nc.sync.dma_start(out=wgs_sb[:, BANK:S], in_=wgs[:, BANK:S])
         load_w1(2)
         load_old(0)
         load_old(1)
@@ -239,15 +256,14 @@ def tile_list_paged_cache_write_kernel(
 
         nc.vector.tensor_copy(v_first[:], table[0][:].indirect(list1[:]))
         nc.vector.tensor_copy(v_scales[:], table_scales[:].indirect(list1[:]))
-        cast_w1(0, nc.scalar.copy)
+        cast_w1(0)
         quantize_w1(0)
         for half in range(HALVES):
-            nc.vector.tensor_copy(v_second[half][:], table[1][:].indirect(entries(list1, half)))
-        first_layer(0, h_banks)
-        cast_w1(1, nc.scalar.copy)
+            nc.vector.tensor_copy(v_words(1, half), table[1][:].indirect(entries(list1, half)))
+        first_layer(0)
+        cast_w1(2)
         quantize_w1(1)
-        first_layer(1, h_banks)
-        cast_w1(2, nc.scalar.copy)
+        first_layer(1)
 
         staged = [wide.tile([P, 2, N_TILES, BANK], F32, name="staged%d" % i, tag="wide", align_bytes=64) for i in range(2)]
 
@@ -258,46 +274,36 @@ def tile_list_paged_cache_write_kernel(
             return bias[:, SLICES + n : SLICES + n + 1]
 
         held = [(0, 0), (0, 1)]
-        parked = [(c, n) for c in range(CHUNKS) for n in range(N_TILES) if n < PARKED[c] and (c, n) not in held]
-        spare_banks = word_banks + h_banks
-
-        def park(i):
-            c, n = parked[i]
-            bank = spare_banks[i % len(spare_banks)]
-            second_layer(bank, c, n, 0, True, True)
-            nc.scalar.activation(out=staging(c, n), in_=bank[:], func=ACT.Identity, bias=out_bias(n))
+        parked = [(0, 2), (0, 3)]
 
         for s in range(SLICES):
             if s + 2 < SLICES:
                 quantize_w1(s + 2)
             scatter(s)
-            if s == 4:
-                for c in range(CHUNKS):
-                    turn_back(0, c, (nc.scalar.copy, nc.scalar.copy))
-                    quantize_z(0, c)
-            if s + 2 < SLICES:
-                first_layer(s + 2, word_banks if s == 4 else h_banks)
             if s + 3 < SLICES:
-                cast_w1(s + 3, nc.scalar.copy)
+                cast_w1(s + 3)
+            if s + 2 < SLICES:
+                first_layer(s + 2)
             for c in range(CHUNKS):
                 turn(old_sb[s % OLD_BUFS], c, True, False)
             if s + OLD_BUFS < SLICES:
                 load_old(s + OLD_BUFS)
-            if s == SLICES - 2:
-                for i in range(len(parked) // 2):
-                    park(i)
-            if s == SLICES - 1:
-                for i in range(len(parked) // 2, len(parked)):
-                    park(i)
-                for c, n in held:
-                    second_layer(h_banks[n], c, n, 0, True, False)
-            for c in range(CHUNKS):
-                turn(pages[s % PAGE_BUFS], c, False, True)
             if s < SLICES - 1:
                 for c in range(CHUNKS):
+                    turn(pages[s % PAGE_BUFS], c, False, True)
                     round_sum(s, c, nc.scalar.copy)
+            if 3 <= s < 3 + CHUNKS:
+                turn_back(0, s - 3, (nc.scalar.copy, nc.scalar.copy))
+                quantize_z(0, s - 3)
 
-        for c in range(CHUNKS):
+        for bank, (c, n) in zip(word_banks, parked):
+            second_layer(bank, c, n, 0, True, True)
+            nc.scalar.activation(out=staging(c, n), in_=bank[:], func=ACT.Identity, bias=out_bias(n))
+        for bank, (c, n) in zip(h_banks, held):
+            second_layer(bank, c, n, 0, True, False)
+
+        def close_sum(c):
+            turn(pages[(SLICES - 1) % PAGE_BUFS], c, False, True)
             round_sum(SLICES - 1, c, nc.scalar.copy if c % 2 == 0 else nc.vector.tensor_copy)
 
         def finish(c):
@@ -311,12 +317,20 @@ def tile_list_paged_cache_write_kernel(
                     if (c, n) not in held:
                         second_layer(bank, c, n, 0, True, False)
                     second_layer(bank, c, n, 1, False, True)
-                    nc.scalar.activation(out=dst, in_=bank[:], func=ACT.Identity, bias=out_bias(n))
+                    if c > 0 and n % 2 == 1:
+                        nc.vector.tensor_scalar_add(dst, bank[:], out_bias(n))
+                    else:
+                        nc.scalar.activation(out=dst, in_=bank[:], func=ACT.Identity, bias=out_bias(n))
                 nc.sync.dma_start(out=out[n * P : (n + 1) * P, c * BANK : (c + 1) * BANK], in_=dst)
 
+        close_sum(0)
+        close_sum(1)
         for c in range(CHUNKS):
-            turn_back(1, c, (nc.scalar.copy, nc.scalar.copy))
+            turn_back(1, c, (nc.scalar.copy, nc.vector.tensor_copy if c == 0 else nc.scalar.copy))
             quantize_z(1, c)
-            if c > 0:
+            if c == 0:
+                close_sum(2)
+                close_sum(3)
+            else:
                 finish(c - 1)
         finish(CHUNKS - 1)

@@ -20,15 +20,16 @@ ALU = mybir.AluOpType
 P = 128
 BANK = 512
 PASSES = 2
+PACK = 4
 SLICES = H // P
+LAST = SLICES - 1
 CHUNKS = T2 // BANK
 N_TILES = N // P
 HALVES = S // BANK
-W1_LOADS = (1, 1, 2, 2, 2)
 PAGE_BUFS = 2
-OLD_BUFS = 4
-H_BUFS = 3
-WOVEN_BUFS = 5
+OLD_BUFS = 3
+H_SLOTS = 4
+H_BYTES = 4 * S
 
 
 def tile_list_paged_cache_write_kernel(
@@ -42,58 +43,77 @@ def tile_list_paged_cache_write_kernel(
         psum = ctx.enter_context(tc.psum_pool(name="psum", bufs=1))
 
         banks = [psum.tile([P, BANK], F32, name="bank%d" % i) for i in range(8)]
-        h_banks = banks[0:2]
-        sum_banks = [banks[2], banks[3], banks[6], banks[7]]
-        word_banks = banks[4:6]
-        out_banks = h_banks + sum_banks
+        fixed_pair, swap_pairs, word_banks = banks[0:2], (banks[2:4], banks[4:6]), banks[6:8]
+
+        def h_banks(s):
+            return swap_pairs[s % 2]
+
+        def sum_banks(s):
+            return fixed_pair + swap_pairs[(s + 1) % 2]
+
+        out_banks = word_banks + swap_pairs[0] + fixed_pair + swap_pairs[1]
 
         def tiles(name, count, shape, dtype):
             return [keep.tile(shape, dtype, name="%s%d" % (name, i), align_bytes=64) for i in range(count)]
 
+        def placed(name, shape, dtype, offset):
+            return reuse.tile(shape, dtype, name=name, align_bytes=64, offset=offset)
+
         list1 = keep.tile([P, S // 16], U16, name="list1")
         list2 = keep.tile([P, S // 16], U16, name="list2")
         table = [wide.tile([P, T], U32, name="table%d" % a, tag="wide", align_bytes=64) for a in range(PASSES)]
-        table_scales = reuse.tile([P, T], U8, name="table_scales", align_bytes=64, offset=1024)
-        v_first = keep.tile([P, S], U32, name="v_first", align_bytes=64)
-        v_second = reuse.tile([P, S], U32, name="v_second", align_bytes=64, offset=2048)
+        table_scales = keep.tile([P, T], U8, name="table_scales", align_bytes=64)
+        v_words = tiles("v_words", PASSES, [P, S], U32)
         v_scales = keep.tile([P, S], U8, name="v_scales", align_bytes=64)
-        w1_raw = [
-            keep.tile([P, PASSES, 4, n * P], F32, name="w1_raw%d" % i, align_bytes=64)
-            if i != 1
-            else reuse.tile([P, PASSES, 4, n * P], F32, name="w1_raw1", align_bytes=64, offset=6144)
-            for i, n in enumerate(W1_LOADS)
+        first_places = (0, (H_SLOTS + 1) * H_BYTES)
+        w1_first = keep.tile([P, PASSES, PACK, P], F32, name="w1_first", align_bytes=64)
+        w1_second = placed("w1_second", [P, PASSES, PACK, P], F32, first_places[1])
+        w1_pair = placed("w1_pair", [P, PASSES, PACK, 2 * P], F32, H_BYTES)
+        w1_dealt = [
+            keep.tile([P, PACK, BANK], F32, name="w1_dealt0", align_bytes=64),
+            keep.tile([P, PACK, BANK], F32, name="w1_dealt1", align_bytes=64),
         ]
-        cast_third = reuse.tile([P, PASSES * P * 4], BF16, name="cast_third", align_bytes=64, offset=8192)
-        h_late = reuse.tile([P, BANK], F32, name="h_late", align_bytes=64, offset=6144)
-        cast_first = keep.tile([P, PASSES * P * 4], BF16, name="cast_first", align_bytes=64)
-        cast_later = reuse.tile([P, PASSES * P * 4], BF16, name="cast_later", align_bytes=64, offset=0)
-        w1_words = [reuse.tile([P, PASSES * P], U32, name="w1_words_first", align_bytes=64, offset=1024)]
-        w1_words.extend(tiles("w1_words", SLICES - 1, [P, PASSES * P], U32))
-        w1_scales = tiles("w1_scales", SLICES, [P, PASSES * P], U8)
-        wgs_sb = keep.tile([P, S], F32, name="wgs_sb")
+        w1_raw = [w1_first[:], w1_second[:], w1_pair[:, :, :, 0:P], w1_pair[:, :, :, P : 2 * P]]
+        cast_plain = tiles("cast_plain", PACK, [P, PASSES * BANK], BF16)
+        cast_dealt = [
+            keep.tile([P, 2, PASSES, BANK], BF16, name="cast_dealt0", align_bytes=64),
+            placed("cast_dealt1", [P, 2, PASSES, BANK], BF16, H_SLOTS * H_BYTES),
+        ]
+        h_first = [placed("h_first%d" % i, [P, BANK], F32, first_places[i]) for i in range(HALVES)]
+        h_sb = [None] + [placed("h_sb%d" % s, [P, S], F32, (s % H_SLOTS) * H_BYTES) for s in range(1, SLICES)]
+        w1_words = tiles("w1_words", 2, [P, PASSES * P], U32)
+        w1_words.extend([placed("w1_words%d" % (i + 2), [P, PASSES * P], U32, first_places[i]) for i in range(HALVES)])
+        w1_words.extend(
+            [placed("w1_words%d" % s, [P, PASSES * P], U32, ((s - 3) % H_SLOTS) * H_BYTES) for s in range(4, SLICES)]
+        )
+        w1_scales = [
+            placed("w1_scales4", [P, PASSES * P], U8, H_SLOTS * H_BYTES)
+            if s == PACK
+            else keep.tile([P, PASSES * P], U8, name="w1_scales%d" % s, align_bytes=64)
+            for s in range(SLICES)
+        ]
+        wgs_plain = keep.tile([P, S], F32, name="wgs_plain")
+        wgs_dealt = keep.tile([P, PACK, S], F32, name="wgs_dealt")
         old_sb = tiles("old_sb", OLD_BUFS, [P, T2], F32)
         pages = tiles("page", PAGE_BUFS, [P, T2 + 1], F32)
-        h_sb = tiles("h_sb", H_BUFS, [P, S], F32)
-        z_turned = tiles("z_turned", PASSES * CHUNKS, [P, 4, 2, 2 * P], BF16)
-        z_woven = tiles("z_woven", WOVEN_BUFS, [P, BANK * 4], BF16)
+        z_turned = tiles("z_turned", CHUNKS, [P, 4, 2, 2 * P], BF16)
+        low_place = (H_SLOTS + 2) * H_BYTES
+        z_low = tiles("z_low", CHUNKS - 1, [P, 4, 2 * P], BF16)
+        z_low.append(placed("z_low_last", [P, 4, 2 * P], BF16, low_place))
+        z_woven = tiles("z_woven", CHUNKS, [P, BANK * PACK], BF16)
         z_words = tiles("z_words", PASSES * CHUNKS, [P, BANK], U32)
         z_scales = tiles("z_scales", PASSES * CHUNKS, [P, BANK], U8)
         w2_sb = keep.tile([P, PASSES, 2 * N], U8, name="w2_sb", align_bytes=64)
         w2_planes = keep.tile([P, PASSES, N], U8, name="w2_planes", align_bytes=64)
         ident = keep.tile([P, P], F32, name="ident")
         bias_rows = keep.tile([P, P], F32, name="bias_rows")
-        bias = keep.tile([P, SLICES + N_TILES], F32, name="bias")
+        bias = keep.tile([P, PACK + N_TILES], F32, name="bias")
+        bias_dealt = keep.tile([P, PACK], F32, name="bias_dealt")
 
-        w1_place = []
-        for i, n in enumerate(W1_LOADS):
-            w1_place.extend([(i, j) for j in range(n)])
-
-        def load_w1(i):
-            first = sum(W1_LOADS[:i]) * P
-            cols = slice(first, first + W1_LOADS[i] * P)
+        def load_w1(raw, first, width):
             for a in range(PASSES):
-                rows = w1[a * BANK : (a + 1) * BANK, cols]
-                nc.sync.dma_start(out=w1_raw[i][:, a], in_=rows.rearrange("(p j) c -> p j c", j=4))
+                rows = w1[a * BANK : (a + 1) * BANK, first : first + width]
+                nc.sync.dma_start(out=raw[:, a], in_=rows.rearrange("(p j) c -> p j c", j=PACK))
 
         def load_table(a):
             nc.sync.dma_start(
@@ -101,73 +121,75 @@ def tile_list_paged_cache_write_kernel(
             )
 
         def load_old(s):
-            nc.sync.dma_start(out=old_sb[s % OLD_BUFS][:], in_=old[s * P : (s + 1) * P, :])
-
-        def w1_cast(s):
-            return {0: cast_first, 2: cast_third}.get(s, cast_later)
+            if s < PACK:
+                rows = old[s * P : (s + 1) * P, :]
+            else:
+                rows = old[BANK:H, :].rearrange("(p t) c -> p t c", t=PACK)[:, s - PACK, :]
+            nc.sync.dma_start(out=old_sb[s % OLD_BUFS][:], in_=rows)
 
         def cast_w1(s):
-            i, j = w1_place[s]
-            raw = w1_raw[i][:, :, :, j * P : (j + 1) * P]
             nc.scalar.copy(
-                out=w1_cast(s)[:].rearrange("p (a c j) -> p a c j", a=PASSES, j=4),
-                in_=raw.rearrange("p a j c -> p a c j"),
+                out=cast_plain[s][:].rearrange("p (a c j) -> p a c j", a=PASSES, j=PACK),
+                in_=w1_raw[s].rearrange("p a j c -> p a c j"),
             )
 
+        def cast_w1_dealt(u):
+            for a in range(PASSES):
+                nc.scalar.copy(
+                    out=cast_dealt[u][:, :, a, :].rearrange("p e (m j) -> p m e j", j=PACK),
+                    in_=w1_dealt[a][:].rearrange("p j (m t) -> p m t j", t=PACK)[:, :, 2 * u : 2 * u + 2, :],
+                )
+
         def quantize_w1(s):
-            nc.vector.quantize_mx(
-                out=w1_words[s][:].bitcast(FP8X4), scales=w1_scales[s][:], in_=w1_cast(s)[:]
-            )
+            src = cast_plain[s][:] if s < PACK else cast_dealt[(s - PACK) // 2][:, s % 2].rearrange("p a w -> p (a w)")
+            nc.vector.quantize_mx(out=w1_words[s][:].bitcast(FP8X4), scales=w1_scales[s][:], in_=src)
 
         def entries(lst, half):
             return lst[:, half * (BANK // 16) : (half + 1) * (BANK // 16)]
 
-        def v_words(a, half):
-            return (v_first if a == 0 else v_second)[:, half * BANK : (half + 1) * BANK]
-
         def h_half(s, half):
-            if s == 0 and half == 1:
-                return h_late[:]
-            return h_sb[s % H_BUFS][:, half * BANK : (half + 1) * BANK]
+            if s == 0:
+                return h_first[half][:]
+            return h_sb[s][:, half * BANK : (half + 1) * BANK]
+
+        def first_product(s, half):
+            entry_cols = slice(half * BANK, (half + 1) * BANK)
+            for a in range(PASSES):
+                cols = slice(a * P, (a + 1) * P)
+                nc.tensor.matmul_mx(
+                    out=h_banks(s)[half][:],
+                    lhsT=w1_words[s][:, cols].bitcast(FP8X4),
+                    lhsT_scale=w1_scales[s][:, cols],
+                    rhs=v_words[a][:, entry_cols].bitcast(FP8X4),
+                    rhs_scale=v_scales[4 * a : P, entry_cols],
+                    start=(a == 0),
+                    stop=(a == PASSES - 1),
+                )
+
+        def relu(s, half):
+            col = bias[:, s : s + 1] if s < PACK else bias_dealt[:, s - PACK : s - PACK + 1]
+            nc.scalar.activation(out=h_half(s, half), in_=h_banks(s)[half][:], func=ACT.Relu, bias=col)
 
         def first_layer(s):
             for half in range(HALVES):
-                for a in range(PASSES):
-                    cols = slice(a * P, (a + 1) * P)
-                    nc.tensor.matmul_mx(
-                        out=h_banks[half][:],
-                        lhsT=w1_words[s][:, cols].bitcast(FP8X4),
-                        lhsT_scale=w1_scales[s][:, cols],
-                        rhs=v_words(a, half).bitcast(FP8X4),
-                        rhs_scale=v_scales[4 * a : P, half * BANK : (half + 1) * BANK],
-                        start=(a == 0),
-                        stop=(a == PASSES - 1),
-                    )
-                if s == 0 and half == 1:
-                    cast_w1(1)
-                nc.scalar.activation(
-                    out=h_half(s, half),
-                    in_=h_banks[half][:],
-                    func=ACT.Relu,
-                    bias=bias[:, s : s + 1],
-                )
+                first_product(s, half)
+                relu(s, half)
 
         def scatter(s):
-            page, h = pages[s % PAGE_BUFS], h_sb[s % H_BUFS]
-            if s == 0:
-                for half in range(HALVES):
-                    cols = slice(half * BANK, (half + 1) * BANK)
-                    nc.vector.tensor_tensor(
-                        page[:].indirect(entries(list2, half)), h_half(s, half), wgs_sb[:, cols], ALU.mult
-                    )
-            else:
-                nc.vector.tensor_tensor(page[:].indirect(list2[:]), h[:], wgs_sb[:], ALU.mult)
+            weight = wgs_plain[:] if s < PACK else wgs_dealt[:, s - PACK, :]
+            nc.vector.tensor_tensor(pages[s % PAGE_BUFS][:].indirect(list2[:]), h_sb[s][:], weight, ALU.mult)
 
-        def turn(src, c, start, stop):
+        def scatter_first(half):
+            cols = slice(half * BANK, (half + 1) * BANK)
+            nc.vector.tensor_tensor(
+                pages[0][:].indirect(entries(list2, half)), h_first[half][:], wgs_plain[:, cols], ALU.mult
+            )
+
+        def turn(s, src, c, start, stop):
             for q in range(4):
                 cols = slice(c * BANK + q * P, c * BANK + (q + 1) * P)
                 nc.tensor.matmul(
-                    sum_banks[c][:, q * P : (q + 1) * P],
+                    sum_banks(s)[c][:, q * P : (q + 1) * P],
                     lhsT=src[:, cols],
                     rhs=ident[:],
                     is_transpose=True,
@@ -175,51 +197,57 @@ def tile_list_paged_cache_write_kernel(
                     stop=(stop and q == 3),
                 )
 
-        def turned(a, c):
-            return z_turned[a * CHUNKS + c]
+        def pair_words(a, c, u):
+            return z_low[c][:] if (a, u) == (1, 0) else z_turned[c][:, :, u, :]
 
-        def round_sum(s, c, copy):
-            a, sq = divmod(s, 4)
-            copy(
-                out=turned(a, c)[:, :, :, sq * 64 : (sq + 1) * 64].rearrange("p q u (m e) -> p u q m e", e=2),
-                in_=sum_banks[c][:].rearrange("p (q m u e) -> p u q m e", q=4, u=2, e=2),
-            )
+        def round_sum(s, c):
+            bank = sum_banks(s)[c]
+            if s < PACK:
+                nc.scalar.copy(
+                    out=z_turned[c][:, :, :, s * 64 : (s + 1) * 64].rearrange("p q u (m e) -> p u q m e", e=2),
+                    in_=bank[:].rearrange("p (q m u e) -> p u q m e", q=4, u=2, e=2),
+                )
+            else:
+                u, e = divmod(s - PACK, 2)
+                nc.scalar.copy(
+                    out=pair_words(1, c, u).rearrange("p q (m e) -> p q m e", e=2)[:, :, :, e],
+                    in_=bank[:].rearrange("p (q m) -> p q m", q=4),
+                )
 
-        def turn_back(a, c, copies):
-            words = turned(a, c)[:].rearrange("p q u w -> p (q u w)").bitcast(F32)
-            woven = z_woven[(a * CHUNKS + c) % WOVEN_BUFS][:].bitcast(F32)
+        def turn_back(a, c):
+            pair = word_banks if a == 0 else out_banks[2 * c : 2 * c + 2]
+            woven = z_woven[c][:].bitcast(F32)
             for b in range(2):
                 for i in range(4):
+                    q, u = 2 * b + i // 2, i % 2
                     nc.tensor.transpose(
-                        word_banks[b][:, i * P : (i + 1) * P],
-                        words[:, (4 * b + i) * P : (4 * b + i + 1) * P],
-                        ident[:],
+                        pair[b][:, i * P : (i + 1) * P], pair_words(a, c, u)[:, q, :].bitcast(F32), ident[:]
                     )
-                copies[b](
+                nc.scalar.copy(
                     out=woven[:, b * BANK : (b + 1) * BANK].rearrange("p (q t u) -> p q t u", q=2, u=2),
-                    in_=word_banks[b][:].rearrange("p (q u t) -> p q t u", q=2, u=2),
+                    in_=pair[b][:].rearrange("p (q u t) -> p q t u", q=2, u=2),
                 )
 
         def quantize_z(a, c):
             i = a * CHUNKS + c
-            nc.vector.quantize_mx(out=z_words[i][:].bitcast(FP8X4), scales=z_scales[i][:], in_=z_woven[i % WOVEN_BUFS][:])
+            nc.vector.quantize_mx(out=z_words[i][:].bitcast(FP8X4), scales=z_scales[i][:], in_=z_woven[c][:])
 
-        def second_layer(bank, c, n, a, start, stop):
+        def second_product(c, n, a):
             nc.tensor.matmul_mx(
-                out=bank[:],
+                out=out_banks[(c * N_TILES + n) % len(out_banks)][:],
                 lhsT=w2_sb[:, a, 2 * n * P : 2 * (n + 1) * P].bitcast(FP4X4),
                 lhsT_scale=w2_planes[:, a, n * P : (n + 1) * P],
                 rhs=z_words[a * CHUNKS + c][:].bitcast(FP8X4),
                 rhs_scale=z_scales[a * CHUNKS + c][:],
-                start=start,
-                stop=stop,
+                start=(a == 0),
+                stop=(a == PASSES - 1),
             )
 
         nc.vector.memset(table_scales[:].bitcast(I32), 0)
         nc.vector.memset(bias_rows[:], 0.0)
         make_identity(nc, ident[:])
         for q in range(4):
-            nc.gpsimd.dma_start(
+            nc.scalar.dma_start(
                 out=table_scales[32 * q : 32 * q + 8, :].bitcast(I32),
                 in_=tab_scales[:, 4 * q : 4 * q + 4, :].bitcast(I32),
             )
@@ -227,23 +255,26 @@ def tile_list_paged_cache_write_kernel(
             nc.vector.memset(page[:], 0.0)
         nc.vector.memset(w2_planes[:].rearrange("p a c -> p (a c)").bitcast(I32), 0)
 
-        nc.scalar.dma_start(out=bias_rows[0:SLICES, :], in_=b1.rearrange("(s p) -> s p", p=P))
-        nc.scalar.dma_start(out=bias_rows[SLICES : SLICES + N_TILES, :], in_=bo.rearrange("(s p) -> s p", p=P))
         nc.sync.dma_start(list1[:], offs)
         load_table(0)
-        load_w1(0)
+        load_w1(w1_first, 0, P)
+        nc.sync.dma_start(out=bias_rows[0:PACK, :], in_=b1[0:BANK].rearrange("(s p) -> s p", p=P))
+        nc.sync.dma_start(out=bias_rows[PACK : PACK + N_TILES, :], in_=bo.rearrange("(s p) -> s p", p=P))
         load_table(1)
         nc.sync.dma_start(list2[:], offs2)
-        nc.sync.dma_start(out=wgs_sb[:, 0:BANK], in_=wgs[:, 0:BANK])
-        load_w1(1)
-        nc.sync.dma_start(out=wgs_sb[:, BANK:S], in_=wgs[:, BANK:S])
-        load_w1(2)
+        nc.sync.dma_start(out=wgs_plain[:, 0:BANK], in_=wgs[:, 0:BANK])
+        load_w1(w1_second, P, P)
+        nc.sync.dma_start(out=wgs_plain[:, BANK:S], in_=wgs[:, BANK:S])
+        load_w1(w1_pair, 2 * P, 2 * P)
+        for a in range(PASSES):
+            rows = w1[a * BANK : (a + 1) * BANK, BANK:H]
+            nc.sync.dma_start(out=w1_dealt[a][:], in_=rows.rearrange("(p j) c -> p j c", j=PACK))
         load_old(0)
         load_old(1)
-        load_w1(3)
+        nc.sync.dma_start(out=bias_dealt[:], in_=b1[BANK:H].rearrange("(p t) -> p t", t=PACK))
         load_old(2)
-        load_w1(4)
-        load_old(3)
+        for q in (0, 2, 1, 3):
+            nc.sync.dma_start(out=wgs_dealt[32 * q : 32 * (q + 1)], in_=wgs.rearrange("(m t) j -> m t j", t=PACK))
         nc.sync.dma_start(out=w2_sb[:].bitcast(I32), in_=w2_words.rearrange("a p c -> p a c").bitcast(I32))
         for q in range(4):
             nc.sync.dma_start(
@@ -252,85 +283,90 @@ def tile_list_paged_cache_write_kernel(
             )
 
         nc.tensor.transpose(word_banks[0][:, 0:P], bias_rows[:], ident[:])
-        nc.scalar.activation(out=bias[:], in_=word_banks[0][:, 0 : SLICES + N_TILES], func=ACT.Identity)
+        nc.scalar.activation(out=bias[:], in_=word_banks[0][:, 0 : PACK + N_TILES], func=ACT.Identity)
 
-        nc.vector.tensor_copy(v_first[:], table[0][:].indirect(list1[:]))
         nc.vector.tensor_copy(v_scales[:], table_scales[:].indirect(list1[:]))
+        nc.vector.tensor_copy(v_words[0][:], table[0][:].indirect(list1[:]))
         cast_w1(0)
         quantize_w1(0)
         for half in range(HALVES):
-            nc.vector.tensor_copy(v_words(1, half), table[1][:].indirect(entries(list1, half)))
-        first_layer(0)
-        cast_w1(2)
+            cols = slice(half * BANK, (half + 1) * BANK)
+            nc.vector.tensor_copy(v_words[1][:, cols], table[1][:].indirect(entries(list1, half)))
+        first_product(0, 0)
+        relu(0, 0)
+        first_product(0, 1)
+        cast_w1(1)
+        relu(0, 1)
         quantize_w1(1)
+        scatter_first(0)
+        cast_w1(2)
+        cast_w1(3)
+        quantize_w1(2)
         first_layer(1)
 
         staged = [wide.tile([P, 2, N_TILES, BANK], F32, name="staged%d" % i, tag="wide", align_bytes=64) for i in range(2)]
+        outputs = [(c, n) for c in range(CHUNKS) for n in range(N_TILES)]
+        held = outputs[0:8]
 
-        def staging(c, n):
-            return staged[c // 2][:, c % 2, n, :]
-
-        def out_bias(n):
-            return bias[:, SLICES + n : SLICES + n + 1]
-
-        held = [(0, 0), (0, 1)]
-        parked = [(0, 2), (0, 3)]
-
-        for s in range(SLICES):
-            if s + 2 < SLICES:
-                quantize_w1(s + 2)
-            scatter(s)
+        for s in range(LAST):
+            if s == 0:
+                scatter_first(1)
+            else:
+                scatter(s)
             if s + 3 < SLICES:
-                cast_w1(s + 3)
+                quantize_w1(s + 3)
             if s + 2 < SLICES:
                 first_layer(s + 2)
+            if s in (0, 2):
+                cast_w1_dealt(s // 2)
             for c in range(CHUNKS):
-                turn(old_sb[s % OLD_BUFS], c, True, False)
-            if s + OLD_BUFS < SLICES:
-                load_old(s + OLD_BUFS)
-            if s < SLICES - 1:
+                turn(s, pages[s % PAGE_BUFS], c, s == 0, s > 0)
+                if s == 0:
+                    continue
+                round_sum(s, c)
+            if s == 0:
                 for c in range(CHUNKS):
-                    turn(pages[s % PAGE_BUFS], c, False, True)
-                    round_sum(s, c, nc.scalar.copy)
-            if 3 <= s < 3 + CHUNKS:
-                turn_back(0, s - 3, (nc.scalar.copy, nc.scalar.copy))
-                quantize_z(0, s - 3)
+                    turn(s, old_sb[0], c, False, True)
+                    round_sum(s, c)
+            if s + 1 < LAST:
+                for c in (2, 3, 0, 1):
+                    turn(s + 1, old_sb[(s + 1) % OLD_BUFS], c, True, False)
+            for later in {0: (3, 4), 1: (5,), 2: (6,), 3: (7,)}.get(s, ()):
+                load_old(later)
+            for c in {3: (0, 1), 4: (2,), 5: (3,)}.get(s, ()):
+                turn_back(0, c)
+                quantize_z(0, c)
 
-        for bank, (c, n) in zip(word_banks, parked):
-            second_layer(bank, c, n, 0, True, True)
-            nc.scalar.activation(out=staging(c, n), in_=bank[:], func=ACT.Identity, bias=out_bias(n))
-        for bank, (c, n) in zip(h_banks, held):
-            second_layer(bank, c, n, 0, True, False)
-
-        def close_sum(c):
-            turn(pages[(SLICES - 1) % PAGE_BUFS], c, False, True)
-            round_sum(SLICES - 1, c, nc.scalar.copy if c % 2 == 0 else nc.vector.tensor_copy)
-
-        def finish(c):
-            for n in range(N_TILES):
-                bank = out_banks[(c * N_TILES + n) % len(out_banks)]
-                dst = staging(c, n)
-                if (c, n) in parked:
-                    second_layer(bank, c, n, 1, True, True)
-                    nc.vector.tensor_tensor(dst, bank[:], dst, ALU.add)
-                else:
-                    if (c, n) not in held:
-                        second_layer(bank, c, n, 0, True, False)
-                    second_layer(bank, c, n, 1, False, True)
-                    if c > 0 and n % 2 == 1:
-                        nc.vector.tensor_scalar_add(dst, bank[:], out_bias(n))
-                    else:
-                        nc.scalar.activation(out=dst, in_=bank[:], func=ACT.Identity, bias=out_bias(n))
-                nc.sync.dma_start(out=out[n * P : (n + 1) * P, c * BANK : (c + 1) * BANK], in_=dst)
-
-        close_sum(0)
-        close_sum(1)
         for c in range(CHUNKS):
-            turn_back(1, c, (nc.scalar.copy, nc.vector.tensor_copy if c == 0 else nc.scalar.copy))
-            quantize_z(1, c)
-            if c == 0:
-                close_sum(2)
-                close_sum(3)
+            turn_back(1, c)
+        for c, n in held:
+            second_product(c, n, 0)
+        scatter(LAST)
+        for i, (first, width) in enumerate(((0, 256), (256, 256), (512, 512), (1024, 512), (1536, 512))):
+            z_last = placed("z_last%d" % i, [P, width], BF16, low_place + (i % 2) * 2 * BANK)
+            c, start = divmod(first, BANK)
+            cols = slice(first, first + width)
+            part = slice(start, start + width)
+            nc.vector.tensor_tensor(
+                z_last[:], pages[LAST % PAGE_BUFS][:, cols], old_sb[LAST % OLD_BUFS][:, cols], ALU.add
+            )
+            nc.vector.tensor_copy(
+                out=z_woven[c][:].rearrange("p (w t) -> p w t", t=PACK)[:, part, PACK - 1], in_=z_last[:]
+            )
+            nc.vector.quantize_mx(
+                out=z_words[CHUNKS + c][:, part].bitcast(FP8X4),
+                scales=z_scales[CHUNKS + c][:, part],
+                in_=z_woven[c][:, PACK * start : PACK * (start + width)],
+            )
+        for c, n in outputs:
+            if (c, n) not in held:
+                second_product(c, n, 0)
+            second_product(c, n, 1)
+            bank = out_banks[(c * N_TILES + n) % len(out_banks)]
+            dst = staged[c // 2][:, c % 2, n, :]
+            col = bias[:, PACK + n : PACK + n + 1]
+            if c == CHUNKS - 1 and n % 2 == 1:
+                nc.vector.tensor_scalar_add(dst, bank[:], col)
             else:
-                finish(c - 1)
-        finish(CHUNKS - 1)
+                nc.scalar.activation(out=dst, in_=bank[:], func=ACT.Identity, bias=col)
+            nc.sync.dma_start(out=out[n * P : (n + 1) * P, c * BANK : (c + 1) * BANK], in_=dst)

@@ -27,7 +27,7 @@ CHUNKS = T2 // BANK
 N_TILES = N // P
 HALVES = S // BANK
 PAGE_BUFS = 2
-OLD_BUFS = 3
+OLD_BUFS = 4
 H_SLOTS = 4
 H_BYTES = 4 * S
 
@@ -62,52 +62,55 @@ def tile_list_paged_cache_write_kernel(
         list1 = keep.tile([P, S // 16], U16, name="list1")
         list2 = keep.tile([P, S // 16], U16, name="list2")
         table = [wide.tile([P, T], U32, name="table%d" % a, tag="wide", align_bytes=64) for a in range(PASSES)]
-        table_scales = keep.tile([P, T], U8, name="table_scales", align_bytes=64)
         v_words = tiles("v_words", PASSES, [P, S], U32)
         v_scales = keep.tile([P, S], U8, name="v_scales", align_bytes=64)
-        first_places = (0, (H_SLOTS + 1) * H_BYTES)
+        late_place = H_SLOTS * H_BYTES
+        low_place = late_place + H_BYTES
+        dealt_place = low_place + 4 * BANK
+        old_place = dealt_place + PASSES * PACK * 4 * BANK
         w1_first = keep.tile([P, PASSES, PACK, P], F32, name="w1_first", align_bytes=64)
-        w1_second = placed("w1_second", [P, PASSES, PACK, P], F32, first_places[1])
+        w1_second = placed("w1_second", [P, PASSES, PACK, P], F32, late_place)
         w1_pair = placed("w1_pair", [P, PASSES, PACK, 2 * P], F32, H_BYTES)
         w1_dealt = [
-            keep.tile([P, PACK, BANK], F32, name="w1_dealt0", align_bytes=64),
-            keep.tile([P, PACK, BANK], F32, name="w1_dealt1", align_bytes=64),
+            placed("w1_dealt%d" % a, [P, PACK, BANK], F32, dealt_place + a * PACK * 4 * BANK) for a in range(PASSES)
         ]
         w1_raw = [w1_first[:], w1_second[:], w1_pair[:, :, :, 0:P], w1_pair[:, :, :, P : 2 * P]]
-        cast_plain = tiles("cast_plain", PACK, [P, PASSES * BANK], BF16)
-        cast_dealt = [
-            keep.tile([P, 2, PASSES, BANK], BF16, name="cast_dealt0", align_bytes=64),
-            placed("cast_dealt1", [P, 2, PASSES, BANK], BF16, H_SLOTS * H_BYTES),
+        w1_cast = tiles("w1_cast", 3, [P, 2, PASSES, BANK], BF16)
+        w1_cast.append(placed("w1_cast3", [P, 2, PASSES, BANK], BF16, old_place + 2 * 4 * T2))
+        w1_words = keep.tile([P, 2, PASSES * P], U32, name="w1_words", align_bytes=64)
+        w1_scales = keep.tile([P, 2, PASSES * P], U8, name="w1_scales", align_bytes=64)
+        first_parts = ((0, BANK // 2), (BANK // 2, BANK // 2), (BANK, BANK))
+        h_first = [
+            placed("h_first%d" % i, [P, width], F32, 4 * first if first < BANK else late_place)
+            for i, (first, width) in enumerate(first_parts)
         ]
-        h_first = [placed("h_first%d" % i, [P, BANK], F32, first_places[i]) for i in range(HALVES)]
         h_sb = [None] + [placed("h_sb%d" % s, [P, S], F32, (s % H_SLOTS) * H_BYTES) for s in range(1, SLICES)]
-        w1_words = tiles("w1_words", 2, [P, PASSES * P], U32)
-        w1_words.extend([placed("w1_words%d" % (i + 2), [P, PASSES * P], U32, first_places[i]) for i in range(HALVES)])
-        w1_words.extend(
-            [placed("w1_words%d" % s, [P, PASSES * P], U32, ((s - 3) % H_SLOTS) * H_BYTES) for s in range(4, SLICES)]
-        )
-        w1_scales = [
-            placed("w1_scales4", [P, PASSES * P], U8, H_SLOTS * H_BYTES)
-            if s == PACK
-            else keep.tile([P, PASSES * P], U8, name="w1_scales%d" % s, align_bytes=64)
-            for s in range(SLICES)
-        ]
-        wgs_plain = keep.tile([P, S], F32, name="wgs_plain")
+        wgs_place = old_place + OLD_BUFS * 4 * T2
+        table_scales = placed("table_scales", [P, T], U8, wgs_place)
+        wgs_plain = placed("wgs_plain", [P, S], F32, wgs_place)
         wgs_dealt = keep.tile([P, PACK, S], F32, name="wgs_dealt")
-        old_sb = tiles("old_sb", OLD_BUFS, [P, T2], F32)
-        pages = tiles("page", PAGE_BUFS, [P, T2 + 1], F32)
+        old_sb = [placed("old_sb%d" % s, [P, T2], F32, old_place + (s % OLD_BUFS) * 4 * T2) for s in range(SLICES)]
+        pages = tiles("page", PAGE_BUFS, [P, T2], F32)
         z_turned = tiles("z_turned", CHUNKS, [P, 4, 2, 2 * P], BF16)
-        low_place = (H_SLOTS + 2) * H_BYTES
         z_low = tiles("z_low", CHUNKS - 1, [P, 4, 2 * P], BF16)
         z_low.append(placed("z_low_last", [P, 4, 2 * P], BF16, low_place))
-        z_woven = tiles("z_woven", CHUNKS, [P, BANK * PACK], BF16)
-        z_words = tiles("z_words", PASSES * CHUNKS, [P, BANK], U32)
-        z_scales = tiles("z_scales", PASSES * CHUNKS, [P, BANK], U8)
+        woven_first = keep.tile([P, CHUNKS, BANK * PACK], BF16, name="woven_first", align_bytes=64)
+        woven_second = [
+            placed("woven_second%d" % c, [P, BANK * PACK], BF16, dealt_place + c * 2 * BANK * PACK) for c in range(CHUNKS)
+        ]
+        early_words = placed("early_words", [P, 2, BANK], U32, (5 % H_SLOTS) * H_BYTES)
+        early_scales = keep.tile([P, 2, BANK], U8, name="early_scales", align_bytes=64)
+        late_words = [placed("late_words%d" % i, [P, BANK], U32, dealt_place + i * 4 * BANK) for i in range(2)]
+        z_words = [early_words[:, 0], early_words[:, 1], late_words[0][:], late_words[1][:]]
+        z_words.extend([t[:] for t in tiles("z_words", CHUNKS, [P, BANK], U32)])
+        z_scales = [early_scales[:, 0], early_scales[:, 1]]
+        z_scales.extend([t[:] for t in tiles("z_scales", CHUNKS + 2, [P, BANK], U8)])
         w2_sb = keep.tile([P, PASSES, 2 * N], U8, name="w2_sb", align_bytes=64)
         w2_planes = keep.tile([P, PASSES, N], U8, name="w2_planes", align_bytes=64)
         ident = keep.tile([P, P], F32, name="ident")
         bias_rows = keep.tile([P, P], F32, name="bias_rows")
-        bias = keep.tile([P, PACK + N_TILES], F32, name="bias")
+        bias = keep.tile([P, PACK], F32, name="bias")
+        bias_out = keep.tile([P, N_TILES], F32, name="bias_out")
         bias_dealt = keep.tile([P, PACK], F32, name="bias_dealt")
 
         def load_w1(raw, first, width):
@@ -125,64 +128,67 @@ def tile_list_paged_cache_write_kernel(
                 rows = old[s * P : (s + 1) * P, :]
             else:
                 rows = old[BANK:H, :].rearrange("(p t) c -> p t c", t=PACK)[:, s - PACK, :]
-            nc.sync.dma_start(out=old_sb[s % OLD_BUFS][:], in_=rows)
+            nc.sync.dma_start(out=old_sb[s][:], in_=rows)
 
         def cast_w1(s):
             nc.scalar.copy(
-                out=cast_plain[s][:].rearrange("p (a c j) -> p a c j", a=PASSES, j=PACK),
+                out=w1_cast[s // 2][:, s % 2].rearrange("p a (c j) -> p a c j", j=PACK),
                 in_=w1_raw[s].rearrange("p a j c -> p a c j"),
             )
 
         def cast_w1_dealt(u):
             for a in range(PASSES):
                 nc.scalar.copy(
-                    out=cast_dealt[u][:, :, a, :].rearrange("p e (m j) -> p m e j", j=PACK),
+                    out=w1_cast[2 + u][:, :, a, :].rearrange("p e (m j) -> p m e j", j=PACK),
                     in_=w1_dealt[a][:].rearrange("p j (m t) -> p m t j", t=PACK)[:, :, 2 * u : 2 * u + 2, :],
                 )
 
-        def quantize_w1(s):
-            src = cast_plain[s][:] if s < PACK else cast_dealt[(s - PACK) // 2][:, s % 2].rearrange("p a w -> p (a w)")
-            nc.vector.quantize_mx(out=w1_words[s][:].bitcast(FP8X4), scales=w1_scales[s][:], in_=src)
+        def quantize_w1(s, count):
+            part = slice(s % 2, s % 2 + count)
+            nc.vector.quantize_mx(
+                out=w1_words[:, part].rearrange("p s w -> p (s w)").bitcast(FP8X4),
+                scales=w1_scales[:, part].rearrange("p s w -> p (s w)"),
+                in_=w1_cast[s // 2][:, part].rearrange("p s a w -> p (s a w)"),
+            )
 
-        def entries(lst, half):
-            return lst[:, half * (BANK // 16) : (half + 1) * (BANK // 16)]
+        def entries(lst, first, width):
+            return lst[:, first // 16 : (first + width) // 16]
 
-        def h_half(s, half):
-            if s == 0:
-                return h_first[half][:]
-            return h_sb[s][:, half * BANK : (half + 1) * BANK]
-
-        def first_product(s, half):
-            entry_cols = slice(half * BANK, (half + 1) * BANK)
+        def first_product(s, bank, first, width):
+            entry_cols = slice(first, first + width)
             for a in range(PASSES):
                 cols = slice(a * P, (a + 1) * P)
                 nc.tensor.matmul_mx(
-                    out=h_banks(s)[half][:],
-                    lhsT=w1_words[s][:, cols].bitcast(FP8X4),
-                    lhsT_scale=w1_scales[s][:, cols],
+                    out=bank[:, 0:width],
+                    lhsT=w1_words[:, s % 2, cols].bitcast(FP8X4),
+                    lhsT_scale=w1_scales[:, s % 2, cols],
                     rhs=v_words[a][:, entry_cols].bitcast(FP8X4),
                     rhs_scale=v_scales[4 * a : P, entry_cols],
                     start=(a == 0),
                     stop=(a == PASSES - 1),
                 )
 
-        def relu(s, half):
+        def relu(s, dst, src):
             col = bias[:, s : s + 1] if s < PACK else bias_dealt[:, s - PACK : s - PACK + 1]
-            nc.scalar.activation(out=h_half(s, half), in_=h_banks(s)[half][:], func=ACT.Relu, bias=col)
+            nc.scalar.activation(out=dst, in_=src, func=ACT.Relu, bias=col)
 
         def first_layer(s):
             for half in range(HALVES):
-                first_product(s, half)
-                relu(s, half)
+                bank = h_banks(s)[half]
+                first_product(s, bank, half * BANK, BANK)
+                relu(s, h_sb[s][:, half * BANK : (half + 1) * BANK], bank[:])
 
         def scatter(s):
             weight = wgs_plain[:] if s < PACK else wgs_dealt[:, s - PACK, :]
             nc.vector.tensor_tensor(pages[s % PAGE_BUFS][:].indirect(list2[:]), h_sb[s][:], weight, ALU.mult)
 
-        def scatter_first(half):
-            cols = slice(half * BANK, (half + 1) * BANK)
+        def scatter_first(i):
+            first, width = first_parts[i]
             nc.vector.tensor_tensor(
-                pages[0][:].indirect(entries(list2, half)), h_first[half][:], wgs_plain[:, cols], ALU.mult
+                pages[0][:].indirect(entries(list2, first, width)),
+                h_first[i][:],
+                wgs_plain[:, first : first + width],
+                ALU.mult,
             )
 
         def turn(s, src, c, start, stop):
@@ -216,7 +222,7 @@ def tile_list_paged_cache_write_kernel(
 
         def turn_back(a, c):
             pair = word_banks if a == 0 else out_banks[2 * c : 2 * c + 2]
-            woven = z_woven[c][:].bitcast(F32)
+            woven = (woven_first[:, c] if a == 0 else woven_second[c][:]).bitcast(F32)
             for b in range(2):
                 for i in range(4):
                     q, u = 2 * b + i // 2, i % 2
@@ -228,17 +234,13 @@ def tile_list_paged_cache_write_kernel(
                     in_=pair[b][:].rearrange("p (q u t) -> p q t u", q=2, u=2),
                 )
 
-        def quantize_z(a, c):
-            i = a * CHUNKS + c
-            nc.vector.quantize_mx(out=z_words[i][:].bitcast(FP8X4), scales=z_scales[i][:], in_=z_woven[c][:])
-
         def second_product(c, n, a):
             nc.tensor.matmul_mx(
                 out=out_banks[(c * N_TILES + n) % len(out_banks)][:],
                 lhsT=w2_sb[:, a, 2 * n * P : 2 * (n + 1) * P].bitcast(FP4X4),
                 lhsT_scale=w2_planes[:, a, n * P : (n + 1) * P],
-                rhs=z_words[a * CHUNKS + c][:].bitcast(FP8X4),
-                rhs_scale=z_scales[a * CHUNKS + c][:],
+                rhs=z_words[a * CHUNKS + c].bitcast(FP8X4),
+                rhs_scale=z_scales[a * CHUNKS + c],
                 start=(a == 0),
                 stop=(a == PASSES - 1),
             )
@@ -251,6 +253,7 @@ def tile_list_paged_cache_write_kernel(
                 out=table_scales[32 * q : 32 * q + 8, :].bitcast(I32),
                 in_=tab_scales[:, 4 * q : 4 * q + 4, :].bitcast(I32),
             )
+        nc.scalar.dma_start(out=bias_rows[0:PACK, :], in_=b1[0:BANK].rearrange("(s p) -> s p", p=P))
         for page in pages:
             nc.vector.memset(page[:], 0.0)
         nc.vector.memset(w2_planes[:].rearrange("p a c -> p (a c)").bitcast(I32), 0)
@@ -258,13 +261,12 @@ def tile_list_paged_cache_write_kernel(
         nc.sync.dma_start(list1[:], offs)
         load_table(0)
         load_w1(w1_first, 0, P)
-        nc.sync.dma_start(out=bias_rows[0:PACK, :], in_=b1[0:BANK].rearrange("(s p) -> s p", p=P))
-        nc.sync.dma_start(out=bias_rows[PACK : PACK + N_TILES, :], in_=bo.rearrange("(s p) -> s p", p=P))
         load_table(1)
-        nc.sync.dma_start(list2[:], offs2)
+        nc.vector.tensor_copy(v_scales[:], table_scales[:].indirect(list1[:]))
         nc.sync.dma_start(out=wgs_plain[:, 0:BANK], in_=wgs[:, 0:BANK])
-        load_w1(w1_second, P, P)
+        nc.sync.dma_start(list2[:], offs2)
         nc.sync.dma_start(out=wgs_plain[:, BANK:S], in_=wgs[:, BANK:S])
+        load_w1(w1_second, P, P)
         load_w1(w1_pair, 2 * P, 2 * P)
         for a in range(PASSES):
             rows = w1[a * BANK : (a + 1) * BANK, BANK:H]
@@ -273,6 +275,7 @@ def tile_list_paged_cache_write_kernel(
         load_old(1)
         nc.sync.dma_start(out=bias_dealt[:], in_=b1[BANK:H].rearrange("(p t) -> p t", t=PACK))
         load_old(2)
+        load_old(3)
         for q in (0, 2, 1, 3):
             nc.sync.dma_start(out=wgs_dealt[32 * q : 32 * (q + 1)], in_=wgs.rearrange("(m t) j -> m t j", t=PACK))
         nc.sync.dma_start(out=w2_sb[:].bitcast(I32), in_=w2_words.rearrange("a p c -> p a c").bitcast(I32))
@@ -283,42 +286,42 @@ def tile_list_paged_cache_write_kernel(
             )
 
         nc.tensor.transpose(word_banks[0][:, 0:P], bias_rows[:], ident[:])
-        nc.scalar.activation(out=bias[:], in_=word_banks[0][:, 0 : PACK + N_TILES], func=ACT.Identity)
+        nc.scalar.activation(out=bias[:], in_=word_banks[0][:, 0:PACK], func=ACT.Identity)
 
-        nc.vector.tensor_copy(v_scales[:], table_scales[:].indirect(list1[:]))
         nc.vector.tensor_copy(v_words[0][:], table[0][:].indirect(list1[:]))
         cast_w1(0)
-        quantize_w1(0)
+        quantize_w1(0, 1)
         for half in range(HALVES):
             cols = slice(half * BANK, (half + 1) * BANK)
-            nc.vector.tensor_copy(v_words[1][:, cols], table[1][:].indirect(entries(list1, half)))
-        first_product(0, 0)
-        relu(0, 0)
-        first_product(0, 1)
-        cast_w1(1)
-        relu(0, 1)
-        quantize_w1(1)
+            nc.vector.tensor_copy(v_words[1][:, cols], table[1][:].indirect(entries(list1, half * BANK, BANK)))
+        for i, bank in enumerate(h_banks(0) + [word_banks[1]]):
+            first, width = first_parts[i]
+            first_product(0, bank, first, width)
+            if i == 2:
+                cast_w1(1)
+            relu(0, h_first[i][:], bank[:, 0:width])
         scatter_first(0)
+        scatter_first(1)
+        quantize_w1(1, 1)
         cast_w1(2)
         cast_w1(3)
-        quantize_w1(2)
         first_layer(1)
+        scatter_first(2)
+        quantize_w1(2, 2)
 
         staged = [wide.tile([P, 2, N_TILES, BANK], F32, name="staged%d" % i, tag="wide", align_bytes=64) for i in range(2)]
         outputs = [(c, n) for c in range(CHUNKS) for n in range(N_TILES)]
         held = outputs[0:8]
 
         for s in range(LAST):
-            if s == 0:
-                scatter_first(1)
-            else:
+            if s > 0:
                 scatter(s)
-            if s + 3 < SLICES:
-                quantize_w1(s + 3)
+            if s in (2, 4):
+                quantize_w1(s + 2, 2)
             if s + 2 < SLICES:
                 first_layer(s + 2)
-            if s in (0, 2):
-                cast_w1_dealt(s // 2)
+            if s == 0:
+                cast_w1_dealt(0)
             for c in range(CHUNKS):
                 turn(s, pages[s % PAGE_BUFS], c, s == 0, s > 0)
                 if s == 0:
@@ -326,16 +329,26 @@ def tile_list_paged_cache_write_kernel(
                 round_sum(s, c)
             if s == 0:
                 for c in range(CHUNKS):
-                    turn(s, old_sb[0], c, False, True)
+                    turn(s, old_sb[s], c, False, True)
                     round_sum(s, c)
             if s + 1 < LAST:
                 for c in (2, 3, 0, 1):
-                    turn(s + 1, old_sb[(s + 1) % OLD_BUFS], c, True, False)
-            for later in {0: (3, 4), 1: (5,), 2: (6,), 3: (7,)}.get(s, ()):
+                    turn(s + 1, old_sb[s + 1], c, True, False)
+            if s == 1:
+                cast_w1_dealt(1)
+                nc.sync.dma_start(out=bias_rows[0:N_TILES, :], in_=bo.rearrange("(s p) -> s p", p=P))
+                nc.tensor.transpose(word_banks[0][:, 0:P], bias_rows[:], ident[:])
+                nc.scalar.activation(out=bias_out[:], in_=word_banks[0][:, 0:N_TILES], func=ACT.Identity)
+            for later in {0: (4, 5), 2: (7,), 4: (6,)}.get(s, ()):
                 load_old(later)
             for c in {3: (0, 1), 4: (2,), 5: (3,)}.get(s, ()):
                 turn_back(0, c)
-                quantize_z(0, c)
+            if s == 5:
+                nc.vector.quantize_mx(
+                    out=early_words[:].rearrange("p c w -> p (c w)").bitcast(FP8X4),
+                    scales=early_scales[:].rearrange("p c w -> p (c w)"),
+                    in_=woven_first[:, 0:2].rearrange("p c w -> p (c w)"),
+                )
 
         for c in range(CHUNKS):
             turn_back(1, c)
@@ -348,24 +361,28 @@ def tile_list_paged_cache_write_kernel(
             cols = slice(first, first + width)
             part = slice(start, start + width)
             nc.vector.tensor_tensor(
-                z_last[:], pages[LAST % PAGE_BUFS][:, cols], old_sb[LAST % OLD_BUFS][:, cols], ALU.add
+                z_last[:], pages[LAST % PAGE_BUFS][:, cols], old_sb[LAST][:, cols], ALU.add
             )
             nc.vector.tensor_copy(
-                out=z_woven[c][:].rearrange("p (w t) -> p w t", t=PACK)[:, part, PACK - 1], in_=z_last[:]
+                out=woven_second[c][:].rearrange("p (w t) -> p w t", t=PACK)[:, part, PACK - 1], in_=z_last[:]
             )
             nc.vector.quantize_mx(
                 out=z_words[CHUNKS + c][:, part].bitcast(FP8X4),
                 scales=z_scales[CHUNKS + c][:, part],
-                in_=z_woven[c][:, PACK * start : PACK * (start + width)],
+                in_=woven_second[c][:, PACK * start : PACK * (start + width)],
             )
+            if c in (1, 2):
+                nc.vector.quantize_mx(
+                    out=z_words[c + 1].bitcast(FP8X4), scales=z_scales[c + 1], in_=woven_first[:, c + 1]
+                )
         for c, n in outputs:
             if (c, n) not in held:
                 second_product(c, n, 0)
             second_product(c, n, 1)
             bank = out_banks[(c * N_TILES + n) % len(out_banks)]
             dst = staged[c // 2][:, c % 2, n, :]
-            col = bias[:, PACK + n : PACK + n + 1]
-            if c == CHUNKS - 1 and n % 2 == 1:
+            col = bias_out[:, n : n + 1]
+            if c * N_TILES + n in (11, 13, 15):
                 nc.vector.tensor_scalar_add(dst, bank[:], col)
             else:
                 nc.scalar.activation(out=dst, in_=bank[:], func=ACT.Identity, bias=col)

@@ -355,7 +355,7 @@ def tile_list_paged_cache_write_kernel(
         for c, n in held:
             second_product(c, n, 0)
         scatter(LAST)
-        for i, (first, width) in enumerate(((0, 256), (256, 256), (512, 512), (1024, 512), (1536, 512))):
+        for i, (first, width) in enumerate(((0, 256), (256, 256), (512, 512), (1024, 512), (1536, 256), (1792, 256))):
             z_last = placed("z_last%d" % i, [P, width], BF16, low_place + (i % 2) * 2 * BANK)
             c, start = divmod(first, BANK)
             cols = slice(first, first + width)
@@ -375,15 +375,53 @@ def tile_list_paged_cache_write_kernel(
                 nc.vector.quantize_mx(
                     out=z_words[c + 1].bitcast(FP8X4), scales=z_scales[c + 1], in_=woven_first[:, c + 1]
                 )
-        for c, n in outputs:
+        for c, n in outputs[:-N_TILES]:
             if (c, n) not in held:
                 second_product(c, n, 0)
             second_product(c, n, 1)
             bank = out_banks[(c * N_TILES + n) % len(out_banks)]
             dst = staged[c // 2][:, c % 2, n, :]
             col = bias_out[:, n : n + 1]
-            if c * N_TILES + n in (11, 13, 15):
-                nc.vector.tensor_scalar_add(dst, bank[:], col)
-            else:
-                nc.scalar.activation(out=dst, in_=bank[:], func=ACT.Identity, bias=col)
-            nc.sync.dma_start(out=out[n * P : (n + 1) * P, c * BANK : (c + 1) * BANK], in_=dst)
+            nc.scalar.activation(out=dst, in_=bank[:], func=ACT.Identity, bias=col)
+            cols = slice(c * BANK, (c + 1) * BANK)
+            if (c, n) in outputs[0:2]:
+                nc.sync.dma_start(out=out[n * P : (n + 1) * P, cols], in_=dst)
+            elif n % 2 == 1:
+                nc.sync.dma_start(
+                    out=out[(n - 1) * P : (n + 1) * P, cols].rearrange("(n p) c -> p n c", p=P),
+                    in_=staged[c // 2][:, c % 2, n - 1 : n + 1, :],
+                )
+        c = CHUNKS - 1
+        for half in range(2):
+            for pair in range(2):
+                bank = out_banks[N_TILES + 2 * half + pair]
+                for a in range(PASSES):
+                    for i in range(4):
+                        n = 2 * pair + i // 2
+                        part = slice(half * 2 * P + (i % 2) * P, half * 2 * P + (i % 2 + 1) * P)
+                        nc.tensor.matmul_mx(
+                            out=bank[:, i * P : (i + 1) * P],
+                            lhsT=w2_sb[:, a, 2 * n * P : 2 * (n + 1) * P].bitcast(FP4X4),
+                            lhsT_scale=w2_planes[:, a, n * P : (n + 1) * P],
+                            rhs=z_words[a * CHUNKS + c][:, part].bitcast(FP8X4),
+                            rhs_scale=z_scales[a * CHUNKS + c][:, part],
+                            start=(a == 0 and i == 0),
+                            stop=(a == PASSES - 1 and i == 3),
+                        )
+                part = slice(half * 2 * P, (half + 1) * 2 * P)
+                cols = slice(c * BANK + half * 2 * P, c * BANK + (half + 1) * 2 * P)
+                for i in range(2):
+                    n = 2 * pair + i
+                    dst = staged[c // 2][:, c % 2, n, part]
+                    src = bank[:, i * 2 * P : (i + 1) * 2 * P]
+                    if pair == 1:
+                        nc.vector.tensor_scalar_add(dst, src, bias_out[:, n : n + 1])
+                    else:
+                        nc.scalar.activation(out=dst, in_=src, func=ACT.Identity, bias=bias_out[:, n : n + 1])
+                    if half == 1:
+                        nc.sync.dma_start(out=out[n * P : (n + 1) * P, cols], in_=dst)
+                if half == 0:
+                    nc.sync.dma_start(
+                        out=out[2 * pair * P : 2 * (pair + 1) * P, cols].rearrange("(n p) c -> p n c", p=P),
+                        in_=staged[c // 2][:, c % 2, 2 * pair : 2 * pair + 2, part],
+                    )

@@ -88,7 +88,7 @@ def tile_list_paged_cache_write_kernel(
         wgs_place = old_place + OLD_BUFS * 4 * T2
         table_scales = placed("table_scales", [P, T], U8, wgs_place)
         wgs_plain = placed("wgs_plain", [P, S], F32, wgs_place)
-        wgs_dealt = keep.tile([P, PACK, S], F32, name="wgs_dealt")
+        wgs_dealt = tiles("wgs_dealt", 2, [P, 2, S], F32)
         old_sb = [placed("old_sb%d" % s, [P, T2], F32, old_place + (s % OLD_BUFS) * 4 * T2) for s in range(SLICES)]
         pages = tiles("page", PAGE_BUFS, [P, T2], F32)
         z_turned = tiles("z_turned", CHUNKS, [P, 4, 2, 2 * P], BF16)
@@ -129,6 +129,11 @@ def tile_list_paged_cache_write_kernel(
             else:
                 rows = old[BANK:H, :].rearrange("(p t) c -> p t c", t=PACK)[:, s - PACK, :]
             nc.sync.dma_start(out=old_sb[s][:], in_=rows)
+
+        def load_wgs_dealt(u):
+            rows = wgs.rearrange("(m t) j -> m t j", t=PACK)[:, 2 * u : 2 * u + 2, :]
+            for q in (0, 2, 1, 3):
+                nc.sync.dma_start(out=wgs_dealt[u][32 * q : 32 * (q + 1)], in_=rows)
 
         def cast_w1(s):
             nc.scalar.copy(
@@ -179,7 +184,7 @@ def tile_list_paged_cache_write_kernel(
                 relu(s, h_sb[s][:, half * BANK : (half + 1) * BANK], bank[:])
 
         def scatter(s):
-            weight = wgs_plain[:] if s < PACK else wgs_dealt[:, s - PACK, :]
+            weight = wgs_plain[:] if s < PACK else wgs_dealt[(s - PACK) // 2][:, s % 2, :]
             nc.vector.tensor_tensor(pages[s % PAGE_BUFS][:].indirect(list2[:]), h_sb[s][:], weight, ALU.mult)
 
         def scatter_first(i):
@@ -274,10 +279,10 @@ def tile_list_paged_cache_write_kernel(
         load_old(0)
         load_old(1)
         nc.sync.dma_start(out=bias_dealt[:], in_=b1[BANK:H].rearrange("(p t) -> p t", t=PACK))
+        load_wgs_dealt(0)
         load_old(2)
         load_old(3)
-        for q in (0, 2, 1, 3):
-            nc.sync.dma_start(out=wgs_dealt[32 * q : 32 * (q + 1)], in_=wgs.rearrange("(m t) j -> m t j", t=PACK))
+        load_wgs_dealt(1)
         nc.sync.dma_start(out=w2_sb[:].bitcast(I32), in_=w2_words.rearrange("a p c -> p a c").bitcast(I32))
         for q in range(4):
             nc.sync.dma_start(

@@ -28,8 +28,6 @@ N_TILES = N // P
 HALVES = S // BANK
 PAGE_BUFS = 2
 OLD_BUFS = 4
-H_SLOTS = 4
-H_BYTES = 4 * S
 
 
 def tile_list_paged_cache_write_kernel(
@@ -38,7 +36,6 @@ def tile_list_paged_cache_write_kernel(
     nc = tc.nc
     with ExitStack() as ctx:
         keep = ctx.enter_context(tc.tile_pool(name="keep", bufs=1))
-        wide = ctx.enter_context(tc.tile_pool(name="wide", bufs=2))
         reuse = ctx.enter_context(tc.tile_pool(name="reuse", bufs=1))
         psum = ctx.enter_context(tc.psum_pool(name="psum", bufs=1))
 
@@ -61,35 +58,39 @@ def tile_list_paged_cache_write_kernel(
 
         list1 = keep.tile([P, S // 16], U16, name="list1")
         list2 = keep.tile([P, S // 16], U16, name="list2")
-        table = [wide.tile([P, T], U32, name="table%d" % a, tag="wide", align_bytes=64) for a in range(PASSES)]
-        v_words = tiles("v_words", PASSES, [P, S], U32)
+        kb = 1024
+        table_place = (0, 28 * kb)
+        h_place = (56 * kb, 4 * kb, 8 * kb, 68 * kb, 56 * kb, 44 * kb - 64, 8 * kb, 68 * kb)
+        old_place = (48 * kb, 60 * kb, 72 * kb, 80 * kb)
+        dealt_place = table_place[1]
+        low_place = 98 * kb
+        table = [placed("table%d" % a, [P, T], U32, table_place[a]) for a in range(PASSES)]
+        table_scales = keep.tile([P, T], U8, name="table_scales", align_bytes=64)
+        v_words = [placed("v_words0", [P, S], U32, 24 * kb), keep.tile([P, S], U32, name="v_words1", align_bytes=64)]
         v_scales = keep.tile([P, S], U8, name="v_scales", align_bytes=64)
-        late_place = H_SLOTS * H_BYTES
-        low_place = late_place + H_BYTES
-        dealt_place = low_place + 4 * BANK
-        old_place = dealt_place + PASSES * PACK * 4 * BANK
-        w1_first = keep.tile([P, PASSES, PACK, P], F32, name="w1_first", align_bytes=64)
-        w1_second = placed("w1_second", [P, PASSES, PACK, P], F32, late_place)
-        w1_pair = placed("w1_pair", [P, PASSES, PACK, 2 * P], F32, H_BYTES)
+        w1_first = placed("w1_first", [P, PASSES, PACK, P], F32, 100 * kb)
+        w1_second = placed("w1_second", [P, PASSES, PACK, P], F32, 12 * kb)
+        w1_pair = placed("w1_pair", [P, PASSES, PACK, 2 * P], F32, 4 * kb)
         w1_dealt = [
             placed("w1_dealt%d" % a, [P, PACK, BANK], F32, dealt_place + a * PACK * 4 * BANK) for a in range(PASSES)
         ]
         w1_raw = [w1_first[:], w1_second[:], w1_pair[:, :, :, 0:P], w1_pair[:, :, :, P : 2 * P]]
-        w1_cast = tiles("w1_cast", 3, [P, 2, PASSES, BANK], BF16)
-        w1_cast.append(placed("w1_cast3", [P, 2, PASSES, BANK], BF16, old_place + 2 * 4 * T2))
+        w1_cast = [
+            placed("w1_cast0", [P, 2, PASSES, BANK], BF16, 78 * kb),
+            placed("w1_cast1", [P, 2, PASSES, BANK], BF16, 94 * kb),
+            keep.tile([P, 2, PASSES, BANK], BF16, name="w1_cast2", align_bytes=64),
+            placed("w1_cast3", [P, 2, PASSES, BANK], BF16, old_place[2]),
+        ]
+        cast_first = placed("cast_first", [P, PASSES, BANK], BF16, 4 * kb)
         w1_words = keep.tile([P, 2, PASSES * P], U32, name="w1_words", align_bytes=64)
         w1_scales = keep.tile([P, 2, PASSES * P], U8, name="w1_scales", align_bytes=64)
         first_parts = ((0, BANK // 2), (BANK // 2, BANK // 2), (BANK, BANK))
-        h_first = [
-            placed("h_first%d" % i, [P, width], F32, 4 * first if first < BANK else late_place)
-            for i, (first, width) in enumerate(first_parts)
-        ]
-        h_sb = [None] + [placed("h_sb%d" % s, [P, S], F32, (s % H_SLOTS) * H_BYTES) for s in range(1, SLICES)]
-        wgs_place = old_place + OLD_BUFS * 4 * T2
-        table_scales = placed("table_scales", [P, T], U8, wgs_place)
-        wgs_plain = placed("wgs_plain", [P, S], F32, wgs_place)
-        wgs_dealt = tiles("wgs_dealt", 2, [P, 2, S], F32)
-        old_sb = [placed("old_sb%d" % s, [P, T2], F32, old_place + (s % OLD_BUFS) * 4 * T2) for s in range(SLICES)]
+        first_place = (56 * kb - 512, 60 * kb - 512, 15 * kb)
+        h_first = [placed("h_first%d" % i, [P, width], F32, first_place[i]) for i, (first, width) in enumerate(first_parts)]
+        h_sb = [None] + [placed("h_sb%d" % s, [P, S], F32, h_place[s]) for s in range(1, SLICES)]
+        wgs_plain = placed("wgs_plain", [P, S], F32, 0)
+        wgs_dealt = [placed("wgs_dealt%d" % u, [P, 2, S], F32, (16 * kb, 88 * kb)[u]) for u in range(2)]
+        old_sb = [placed("old_sb%d" % s, [P, T2], F32, old_place[s % OLD_BUFS]) for s in range(SLICES)]
         pages = tiles("page", PAGE_BUFS, [P, T2], F32)
         z_turned = tiles("z_turned", CHUNKS, [P, 4, 2, 2 * P], BF16)
         z_low = tiles("z_low", CHUNKS - 1, [P, 4, 2 * P], BF16)
@@ -98,20 +99,20 @@ def tile_list_paged_cache_write_kernel(
         woven_second = [
             placed("woven_second%d" % c, [P, BANK * PACK], BF16, dealt_place + c * 2 * BANK * PACK) for c in range(CHUNKS)
         ]
-        early_words = placed("early_words", [P, 2, BANK], U32, (5 % H_SLOTS) * H_BYTES)
+        early_words = placed("early_words", [P, 2, BANK], U32, 44 * kb)
         early_scales = keep.tile([P, 2, BANK], U8, name="early_scales", align_bytes=64)
         late_words = [placed("late_words%d" % i, [P, BANK], U32, dealt_place + i * 4 * BANK) for i in range(2)]
         z_words = [early_words[:, 0], early_words[:, 1], late_words[0][:], late_words[1][:]]
         z_words.extend([t[:] for t in tiles("z_words", CHUNKS, [P, BANK], U32)])
         z_scales = [early_scales[:, 0], early_scales[:, 1]]
         z_scales.extend([t[:] for t in tiles("z_scales", CHUNKS + 2, [P, BANK], U8)])
-        w2_sb = keep.tile([P, PASSES, 2 * N], U8, name="w2_sb", align_bytes=64)
+        w2_sb = placed("w2_sb", [P, PASSES, 2 * N], U8, 96 * kb)
         w2_planes = keep.tile([P, PASSES, N], U8, name="w2_planes", align_bytes=64)
         ident = keep.tile([P, P], F32, name="ident")
         bias_rows = keep.tile([P, P], F32, name="bias_rows")
         bias = keep.tile([P, PACK], F32, name="bias")
         bias_out = keep.tile([P, N_TILES], F32, name="bias_out")
-        bias_dealt = keep.tile([P, PACK], F32, name="bias_dealt")
+        bias_dealt = placed("bias_dealt", [P, PACK], F32, 100 * kb)
 
         def load_w1(raw, first, width):
             for a in range(PASSES):
@@ -136,8 +137,9 @@ def tile_list_paged_cache_write_kernel(
                 nc.sync.dma_start(out=wgs_dealt[u][32 * q : 32 * (q + 1)], in_=rows)
 
         def cast_w1(s):
+            dst = cast_first[:] if s == 0 else w1_cast[s // 2][:, s % 2]
             nc.scalar.copy(
-                out=w1_cast[s // 2][:, s % 2].rearrange("p a (c j) -> p a c j", j=PACK),
+                out=dst.rearrange("p a (c j) -> p a c j", j=PACK),
                 in_=w1_raw[s].rearrange("p a j c -> p a c j"),
             )
 
@@ -150,10 +152,11 @@ def tile_list_paged_cache_write_kernel(
 
         def quantize_w1(s, count):
             part = slice(s % 2, s % 2 + count)
+            src = cast_first[:].rearrange("p a w -> p (a w)") if s == 0 else None
             nc.vector.quantize_mx(
                 out=w1_words[:, part].rearrange("p s w -> p (s w)").bitcast(FP8X4),
                 scales=w1_scales[:, part].rearrange("p s w -> p (s w)"),
-                in_=w1_cast[s // 2][:, part].rearrange("p s a w -> p (s a w)"),
+                in_=src if s == 0 else w1_cast[s // 2][:, part].rearrange("p s a w -> p (s a w)"),
             )
 
         def entries(lst, first, width):
@@ -250,55 +253,48 @@ def tile_list_paged_cache_write_kernel(
                 stop=(a == PASSES - 1),
             )
 
+        nc.gpsimd.memset(bias_rows[:], 0.0)
         nc.vector.memset(table_scales[:].bitcast(I32), 0)
-        nc.vector.memset(bias_rows[:], 0.0)
+        nc.vector.memset(w2_planes[:].rearrange("p a c -> p (a c)").bitcast(I32), 0)
         make_identity(nc, ident[:])
         for q in range(4):
             nc.scalar.dma_start(
                 out=table_scales[32 * q : 32 * q + 8, :].bitcast(I32),
                 in_=tab_scales[:, 4 * q : 4 * q + 4, :].bitcast(I32),
             )
-        nc.scalar.dma_start(out=bias_rows[0:PACK, :], in_=b1[0:BANK].rearrange("(s p) -> s p", p=P))
-        for page in pages:
-            nc.vector.memset(page[:], 0.0)
-        nc.vector.memset(w2_planes[:].rearrange("p a c -> p (a c)").bitcast(I32), 0)
-
-        nc.sync.dma_start(list1[:], offs)
-        load_table(0)
-        load_w1(w1_first, 0, P)
-        load_table(1)
-        nc.vector.tensor_copy(v_scales[:], table_scales[:].indirect(list1[:]))
-        nc.sync.dma_start(out=wgs_plain[:, 0:BANK], in_=wgs[:, 0:BANK])
-        nc.sync.dma_start(list2[:], offs2)
-        nc.sync.dma_start(out=wgs_plain[:, BANK:S], in_=wgs[:, BANK:S])
-        load_w1(w1_second, P, P)
-        load_w1(w1_pair, 2 * P, 2 * P)
-        for a in range(PASSES):
-            rows = w1[a * BANK : (a + 1) * BANK, BANK:H]
-            nc.sync.dma_start(out=w1_dealt[a][:], in_=rows.rearrange("(p j) c -> p j c", j=PACK))
-        load_old(0)
-        load_old(1)
-        nc.sync.dma_start(out=bias_dealt[:], in_=b1[BANK:H].rearrange("(p t) -> p t", t=PACK))
-        load_wgs_dealt(0)
-        load_old(2)
-        load_old(3)
-        load_wgs_dealt(1)
-        nc.sync.dma_start(out=w2_sb[:].bitcast(I32), in_=w2_words.rearrange("a p c -> p a c").bitcast(I32))
         for q in range(4):
-            nc.sync.dma_start(
+            nc.gpsimd.dma_start(
                 out=w2_planes[32 * q : 32 * q + 4].bitcast(I32),
                 in_=w2_scales[:, 4 * q : 4 * q + 4, :].rearrange("a r c -> r a c").bitcast(I32),
             )
+        for page in pages:
+            nc.vector.memset(page[:], 0.0)
+
+        nc.sync.dma_start(list1[:], offs)
+        load_table(0)
+        nc.sync.dma_start(out=bias_rows[0:PACK, :], in_=b1[0:BANK].rearrange("(s p) -> s p", p=P))
+        load_w1(w1_first, 0, P)
+        load_table(1)
+        nc.sync.dma_start(list2[:], offs2)
 
         nc.tensor.transpose(word_banks[0][:, 0:P], bias_rows[:], ident[:])
         nc.scalar.activation(out=bias[:], in_=word_banks[0][:, 0:PACK], func=ACT.Identity)
 
         nc.vector.tensor_copy(v_words[0][:], table[0][:].indirect(list1[:]))
+        nc.vector.tensor_copy(v_scales[:], table_scales[:].indirect(list1[:]))
+        nc.sync.dma_start(out=wgs_plain[:, 0:BANK], in_=wgs[:, 0:BANK])
+        load_w1(w1_second, P, P)
+        nc.sync.dma_start(out=wgs_plain[:, BANK:S], in_=wgs[:, BANK:S])
         cast_w1(0)
         quantize_w1(0, 1)
-        for half in range(HALVES):
-            cols = slice(half * BANK, (half + 1) * BANK)
-            nc.vector.tensor_copy(v_words[1][:, cols], table[1][:].indirect(entries(list1, half * BANK, BANK)))
+        load_w1(w1_pair, 2 * P, 2 * P)
+        for first, width in first_parts:
+            nc.vector.tensor_copy(
+                v_words[1][:, first : first + width], table[1][:].indirect(entries(list1, first, width))
+            )
+        for a in range(PASSES):
+            rows = w1[a * BANK : (a + 1) * BANK, BANK:H]
+            nc.sync.dma_start(out=w1_dealt[a][:], in_=rows.rearrange("(p j) c -> p j c", j=PACK))
         for i, bank in enumerate(h_banks(0) + [word_banks[1]]):
             first, width = first_parts[i]
             first_product(0, bank, first, width)
@@ -313,8 +309,19 @@ def tile_list_paged_cache_write_kernel(
         first_layer(1)
         scatter_first(2)
         quantize_w1(2, 2)
+        nc.sync.dma_start(out=bias_dealt[:], in_=b1[BANK:H].rearrange("(p t) -> p t", t=PACK))
+        load_old(0)
+        load_old(1)
+        load_old(2)
+        load_old(3)
+        load_wgs_dealt(0)
+        load_wgs_dealt(1)
+        nc.sync.dma_start(out=w2_sb[:].bitcast(I32), in_=w2_words.rearrange("a p c -> p a c").bitcast(I32))
 
-        staged = [wide.tile([P, 2, N_TILES, BANK], F32, name="staged%d" % i, tag="wide", align_bytes=64) for i in range(2)]
+        staged = [
+            placed("staged%d" % c, [P, N_TILES, BANK], F32, (old_place[0], old_place[1], old_place[2], 0)[c])
+            for c in range(CHUNKS)
+        ]
         outputs = [(c, n) for c in range(CHUNKS) for n in range(N_TILES)]
         held = outputs[0:8]
 
@@ -385,7 +392,7 @@ def tile_list_paged_cache_write_kernel(
                 second_product(c, n, 0)
             second_product(c, n, 1)
             bank = out_banks[(c * N_TILES + n) % len(out_banks)]
-            dst = staged[c // 2][:, c % 2, n, :]
+            dst = staged[c][:, n, :]
             col = bias_out[:, n : n + 1]
             nc.scalar.activation(out=dst, in_=bank[:], func=ACT.Identity, bias=col)
             cols = slice(c * BANK, (c + 1) * BANK)
@@ -394,7 +401,7 @@ def tile_list_paged_cache_write_kernel(
             elif n % 2 == 1:
                 nc.sync.dma_start(
                     out=out[(n - 1) * P : (n + 1) * P, cols].rearrange("(n p) c -> p n c", p=P),
-                    in_=staged[c // 2][:, c % 2, n - 1 : n + 1, :],
+                    in_=staged[c][:, n - 1 : n + 1, :],
                 )
         c = CHUNKS - 1
         for half in range(2):
@@ -417,7 +424,7 @@ def tile_list_paged_cache_write_kernel(
                 cols = slice(c * BANK + half * 2 * P, c * BANK + (half + 1) * 2 * P)
                 for i in range(2):
                     n = 2 * pair + i
-                    dst = staged[c // 2][:, c % 2, n, part]
+                    dst = staged[c][:, n, part]
                     src = bank[:, i * 2 * P : (i + 1) * 2 * P]
                     if pair == 1:
                         nc.vector.tensor_scalar_add(dst, src, bias_out[:, n : n + 1])
@@ -428,5 +435,5 @@ def tile_list_paged_cache_write_kernel(
                 if half == 0:
                     nc.sync.dma_start(
                         out=out[2 * pair * P : 2 * (pair + 1) * P, cols].rearrange("(n p) c -> p n c", p=P),
-                        in_=staged[c // 2][:, c % 2, 2 * pair : 2 * pair + 2, part],
+                        in_=staged[c][:, 2 * pair : 2 * pair + 2, part],
                     )

@@ -63,7 +63,7 @@ def tile_list_paged_cache_write_kernel(
         h_place = (56 * kb, 4 * kb, 8 * kb, 68 * kb, 56 * kb, 44 * kb - 64, 8 * kb, 68 * kb)
         old_place = (48 * kb, 60 * kb, 72 * kb, 80 * kb)
         dealt_place = table_place[1]
-        low_place = 98 * kb
+        low_place = 104 * kb
         table = [placed("table%d" % a, [P, T], U32, table_place[a]) for a in range(PASSES)]
         table_scales = keep.tile([P, T], U8, name="table_scales", align_bytes=64)
         v_words = [placed("v_words0", [P, S], U32, 24 * kb), keep.tile([P, S], U32, name="v_words1", align_bytes=64)]
@@ -77,7 +77,7 @@ def tile_list_paged_cache_write_kernel(
         w1_raw = [w1_first[:], w1_second[:], w1_pair[:, :, :, 0:P], w1_pair[:, :, :, P : 2 * P]]
         w1_cast = [
             placed("w1_cast0", [P, 2, PASSES, BANK], BF16, 78 * kb),
-            placed("w1_cast1", [P, 2, PASSES, BANK], BF16, 94 * kb),
+            placed("w1_cast1", [P, 2, PASSES, BANK], BF16, 95 * kb),
             keep.tile([P, 2, PASSES, BANK], BF16, name="w1_cast2", align_bytes=64),
             placed("w1_cast3", [P, 2, PASSES, BANK], BF16, old_place[2]),
         ]
@@ -106,8 +106,9 @@ def tile_list_paged_cache_write_kernel(
         z_words.extend([t[:] for t in tiles("z_words", CHUNKS, [P, BANK], U32)])
         z_scales = [early_scales[:, 0], early_scales[:, 1]]
         z_scales.extend([t[:] for t in tiles("z_scales", CHUNKS + 2, [P, BANK], U8)])
-        w2_sb = placed("w2_sb", [P, PASSES, 2 * N], U8, 96 * kb)
-        w2_planes = keep.tile([P, PASSES, N], U8, name="w2_planes", align_bytes=64)
+        w2_sb = placed("w2_sb", [P, PASSES, 2 * N], U8, 98 * kb)
+        w2_planes = placed("w2_planes", [P, PASSES, N], U8, 97 * kb)
+        bo_rows = placed("bo_rows", [P, P], F32, 96 * kb)
         ident = keep.tile([P, P], F32, name="ident")
         bias_rows = keep.tile([P, P], F32, name="bias_rows")
         bias = keep.tile([P, PACK], F32, name="bias")
@@ -255,17 +256,11 @@ def tile_list_paged_cache_write_kernel(
 
         nc.gpsimd.memset(bias_rows[:], 0.0)
         nc.vector.memset(table_scales[:].bitcast(I32), 0)
-        nc.vector.memset(w2_planes[:].rearrange("p a c -> p (a c)").bitcast(I32), 0)
         make_identity(nc, ident[:])
         for q in range(4):
             nc.scalar.dma_start(
                 out=table_scales[32 * q : 32 * q + 8, :].bitcast(I32),
                 in_=tab_scales[:, 4 * q : 4 * q + 4, :].bitcast(I32),
-            )
-        for q in range(4):
-            nc.gpsimd.dma_start(
-                out=w2_planes[32 * q : 32 * q + 4].bitcast(I32),
-                in_=w2_scales[:, 4 * q : 4 * q + 4, :].rearrange("a r c -> r a c").bitcast(I32),
             )
         for page in pages:
             nc.vector.memset(page[:], 0.0)
@@ -282,9 +277,8 @@ def tile_list_paged_cache_write_kernel(
 
         nc.vector.tensor_copy(v_words[0][:], table[0][:].indirect(list1[:]))
         nc.vector.tensor_copy(v_scales[:], table_scales[:].indirect(list1[:]))
-        nc.sync.dma_start(out=wgs_plain[:, 0:BANK], in_=wgs[:, 0:BANK])
+        nc.sync.dma_start(out=wgs_plain[:], in_=wgs)
         load_w1(w1_second, P, P)
-        nc.sync.dma_start(out=wgs_plain[:, BANK:S], in_=wgs[:, BANK:S])
         cast_w1(0)
         quantize_w1(0, 1)
         load_w1(w1_pair, 2 * P, 2 * P)
@@ -317,6 +311,12 @@ def tile_list_paged_cache_write_kernel(
         load_wgs_dealt(0)
         load_wgs_dealt(1)
         nc.sync.dma_start(out=w2_sb[:].bitcast(I32), in_=w2_words.rearrange("a p c -> p a c").bitcast(I32))
+        nc.gpsimd.memset(w2_planes[:].rearrange("p a c -> p (a c)").bitcast(I32), 0)
+        for q in range(4):
+            nc.sync.dma_start(
+                out=w2_planes[32 * q : 32 * q + 4].bitcast(I32),
+                in_=w2_scales[:, 4 * q : 4 * q + 4, :].rearrange("a r c -> r a c").bitcast(I32),
+            )
 
         staged = [
             placed("staged%d" % c, [P, N_TILES, BANK], F32, (old_place[0], old_place[1], old_place[2], 0)[c])
@@ -348,8 +348,9 @@ def tile_list_paged_cache_write_kernel(
                     turn(s + 1, old_sb[s + 1], c, True, False)
             if s == 1:
                 cast_w1_dealt(1)
-                nc.sync.dma_start(out=bias_rows[0:N_TILES, :], in_=bo.rearrange("(s p) -> s p", p=P))
-                nc.tensor.transpose(word_banks[0][:, 0:P], bias_rows[:], ident[:])
+                nc.gpsimd.memset(bo_rows[:], 0.0)
+                nc.sync.dma_start(out=bo_rows[0:N_TILES, :], in_=bo.rearrange("(s p) -> s p", p=P))
+                nc.tensor.transpose(word_banks[0][:, 0:P], bo_rows[:], ident[:])
                 nc.scalar.activation(out=bias_out[:], in_=word_banks[0][:, 0:N_TILES], func=ACT.Identity)
             for later in {0: (4, 5), 2: (7,), 4: (6,)}.get(s, ()):
                 load_old(later)

@@ -28,6 +28,7 @@ N_TILES = N // P
 HALVES = S // BANK
 PAGE_BUFS = 2
 OLD_BUFS = 4
+SCALE_ROWS_AT = 96
 
 
 def tile_list_paged_cache_write_kernel(
@@ -54,7 +55,8 @@ def tile_list_paged_cache_write_kernel(
             return [keep.tile(shape, dtype, name="%s%d" % (name, i), align_bytes=64) for i in range(count)]
 
         def placed(name, shape, dtype, offset):
-            return reuse.tile(shape, dtype, name=name, align_bytes=64, offset=offset)
+            shift = 9 * 1024 if offset >= 28 * 1024 else 0
+            return reuse.tile(shape, dtype, name=name, align_bytes=64, offset=offset + shift)
 
         list1 = keep.tile([P, S // 16], U16, name="list1")
         list2 = keep.tile([P, S // 16], U16, name="list2")
@@ -65,7 +67,8 @@ def tile_list_paged_cache_write_kernel(
         dealt_place = table_place[1]
         low_place = 104 * kb
         table = [placed("table%d" % a, [P, T], U32, table_place[a]) for a in range(PASSES)]
-        table_scales = keep.tile([P, T], U8, name="table_scales", align_bytes=64)
+        table_scales = reuse.tile([P, T], U8, name="table_scales", align_bytes=64, offset=33 * kb + 512)
+        picked_scales = keep.tile([P, S], U8, name="picked_scales", align_bytes=64)
         v_words = [placed("v_words0", [P, S], U32, 24 * kb), keep.tile([P, S], U32, name="v_words1", align_bytes=64)]
         v_scales = keep.tile([P, S], U8, name="v_scales", align_bytes=64)
         w1_first = placed("w1_first", [P, PASSES, PACK, P], F32, 100 * kb)
@@ -91,7 +94,8 @@ def tile_list_paged_cache_write_kernel(
         wgs_plain = placed("wgs_plain", [P, S], F32, 0)
         wgs_dealt = [placed("wgs_dealt%d" % u, [P, 2, S], F32, (16 * kb, 88 * kb)[u]) for u in range(2)]
         old_sb = [placed("old_sb%d" % s, [P, T2], F32, old_place[s % OLD_BUFS]) for s in range(SLICES)]
-        pages = tiles("page", PAGE_BUFS, [P, T2], F32)
+        pages = tiles("page", 1, [P, T2], F32)
+        pages.append(reuse.tile([P, T2], F32, name="page1", align_bytes=64, offset=28 * kb))
         z_turned = tiles("z_turned", CHUNKS, [P, 4, 2, 2 * P], BF16)
         z_low = tiles("z_low", CHUNKS - 1, [P, 4, 2 * P], BF16)
         z_low.append(placed("z_low_last", [P, 4, 2 * P], BF16, low_place))
@@ -254,29 +258,40 @@ def tile_list_paged_cache_write_kernel(
                 stop=(a == PASSES - 1),
             )
 
-        nc.gpsimd.memset(bias_rows[:], 0.0)
-        nc.vector.memset(table_scales[:].bitcast(I32), 0)
-        make_identity(nc, ident[:])
-        for q in range(4):
-            nc.scalar.dma_start(
-                out=table_scales[32 * q : 32 * q + 8, :].bitcast(I32),
-                in_=tab_scales[:, 4 * q : 4 * q + 4, :].bitcast(I32),
+        def move_scales(a, q):
+            first = SCALE_ROWS_AT + 16 * a + 4 * q
+            nc.sync.dma_start(
+                out=v_scales[32 * q + 4 * a : 32 * q + 4 * a + 4, :].bitcast(I32),
+                in_=picked_scales[first : first + 4, :].bitcast(I32),
             )
-        for page in pages:
-            nc.vector.memset(page[:], 0.0)
+
+        nc.gpsimd.memset(bias_rows[:], 0.0)
+        nc.vector.memset(table_scales[0:SCALE_ROWS_AT, :].bitcast(I32), 0)
+        nc.vector.memset(v_scales[:].bitcast(I32), 0)
+        make_identity(nc, ident[:])
+        nc.vector.memset(pages[0][:], 0.0)
 
         nc.sync.dma_start(list1[:], offs)
+        nc.sync.dma_start(
+            out=table_scales[SCALE_ROWS_AT:P, :].bitcast(I32), in_=tab_scales.rearrange("a r t -> (a r) t").bitcast(I32)
+        )
         load_table(0)
         nc.sync.dma_start(out=bias_rows[0:PACK, :], in_=b1[0:BANK].rearrange("(s p) -> s p", p=P))
         load_w1(w1_first, 0, P)
-        load_table(1)
         nc.sync.dma_start(list2[:], offs2)
+        nc.vector.tensor_copy(picked_scales[:], table_scales[:].indirect(list1[:]))
+        nc.vector.memset(pages[1][:], 0.0)
+        moves = [(a, q) for a in range(PASSES) for q in range(4)]
+        for a, q in moves[:2]:
+            move_scales(a, q)
+        load_table(1)
+        for a, q in moves[2:]:
+            move_scales(a, q)
 
         nc.tensor.transpose(word_banks[0][:, 0:P], bias_rows[:], ident[:])
         nc.scalar.activation(out=bias[:], in_=word_banks[0][:, 0:PACK], func=ACT.Identity)
 
         nc.vector.tensor_copy(v_words[0][:], table[0][:].indirect(list1[:]))
-        nc.vector.tensor_copy(v_scales[:], table_scales[:].indirect(list1[:]))
         nc.sync.dma_start(out=wgs_plain[:], in_=wgs)
         load_w1(w1_second, P, P)
         cast_w1(0)

@@ -292,8 +292,9 @@ def tile_list_paged_cache_write_kernel(
         nc.scalar.activation(out=bias[:], in_=word_banks[0][:, 0:PACK], func=ACT.Identity)
 
         nc.vector.tensor_copy(v_words[0][:], table[0][:].indirect(list1[:]))
-        nc.sync.dma_start(out=wgs_plain[:], in_=wgs)
+        nc.sync.dma_start(out=wgs_plain[:, 0:BANK], in_=wgs[:, 0:BANK])
         load_w1(w1_second, P, P)
+        nc.sync.dma_start(out=wgs_plain[:, BANK:S], in_=wgs[:, BANK:S])
         cast_w1(0)
         quantize_w1(0, 1)
         load_w1(w1_pair, 2 * P, 2 * P)
@@ -424,17 +425,17 @@ def tile_list_paged_cache_write_kernel(
             for pair in range(2):
                 bank = out_banks[N_TILES + 2 * half + pair]
                 for a in range(PASSES):
-                    for i in range(4):
-                        n = 2 * pair + i // 2
-                        part = slice(half * 2 * P + (i % 2) * P, half * 2 * P + (i % 2 + 1) * P)
+                    for i in range(2):
+                        n = 2 * pair + i
+                        part = slice(half * 2 * P, (half + 1) * 2 * P)
                         nc.tensor.matmul_mx(
-                            out=bank[:, i * P : (i + 1) * P],
+                            out=bank[:, i * 2 * P : (i + 1) * 2 * P],
                             lhsT=w2_sb[:, a, 2 * n * P : 2 * (n + 1) * P].bitcast(FP4X4),
                             lhsT_scale=w2_planes[:, a, n * P : (n + 1) * P],
                             rhs=z_words[a * CHUNKS + c][:, part].bitcast(FP8X4),
                             rhs_scale=z_scales[a * CHUNKS + c][:, part],
                             start=(a == 0 and i == 0),
-                            stop=(a == PASSES - 1 and i == 3),
+                            stop=(a == PASSES - 1 and i == 1),
                         )
                 part = slice(half * 2 * P, (half + 1) * 2 * P)
                 cols = slice(c * BANK + half * 2 * P, c * BANK + (half + 1) * 2 * P)

from contextlib import ExitStack

import concourse.mybir as mybir
from concourse.masks import make_identity

K, T, S, H, T2, N = 1024, 4096, 1024, 1024, 2048, 512
FLOPS = 2 * K * H * S + 2 * H * N * T2

F32 = mybir.dt.float32
BF16 = mybir.dt.bfloat16
I32 = mybir.dt.int32
U32 = mybir.dt.uint32
U16 = mybir.dt.uint16
U8 = mybir.dt.uint8
FP8X4 = mybir.dt.float8_e4m3fn_x4
FP4X4 = mybir.dt.float4_e2m1fn_x4
ACT = mybir.ActivationFunctionType
ALU = mybir.AluOpType

P = 128
BANK = 512
PASSES = 2
PACK = 4
SLICES = H // P
LAST = SLICES - 1
CHUNKS = T2 // BANK
N_TILES = N // P
HALVES = S // BANK
PAGE_BUFS = 2
OLD_BUFS = 4
SCALE_ROWS_AT = 96


def tile_list_paged_cache_write_kernel(
    tc, tab_words, tab_scales, offs, w1, b1, wgs, offs2, old, w2_words, w2_scales, bo, out
):
    nc = tc.nc
    with ExitStack() as ctx:
        keep = ctx.enter_context(tc.tile_pool(name="keep", bufs=1))
        reuse = ctx.enter_context(tc.tile_pool(name="reuse", bufs=1))
        psum = ctx.enter_context(tc.psum_pool(name="psum", bufs=1))

        banks = [psum.tile([P, BANK], F32, name="bank%d" % i) for i in range(8)]
        fixed_pair, swap_pairs, word_banks = banks[0:2], (banks[2:4], banks[4:6]), banks[6:8]

        def h_banks(s):
            return swap_pairs[s % 2]

        def sum_banks(s):
            return fixed_pair + swap_pairs[(s + 1) % 2]

        out_banks = word_banks + swap_pairs[0] + fixed_pair + swap_pairs[1]

        def tiles(name, count, shape, dtype):
            return [keep.tile(shape, dtype, name="%s%d" % (name, i), align_bytes=64) for i in range(count)]

        def placed(name, shape, dtype, offset):
            shift = 9 * 1024 if offset >= 28 * 1024 else 0
            return reuse.tile(shape, dtype, name=name, align_bytes=64, offset=offset + shift)

        list1 = keep.tile([P, S // 16], U16, name="list1")
        list2 = keep.tile([P, S // 16], U16, name="list2")
        kb = 1024
        table_place = (0, 28 * kb)
        h_place = (56 * kb, 4 * kb, 8 * kb, 68 * kb, 56 * kb, 44 * kb - 64, 8 * kb, 68 * kb)
        old_place = (48 * kb, 60 * kb, 72 * kb, 80 * kb)
        dealt_place = table_place[1]
        low_place = 104 * kb
        table = [placed("table%d" % a, [P, T], U32, table_place[a]) for a in range(PASSES)]
        table_scales = reuse.tile([P, T], U8, name="table_scales", align_bytes=64, offset=33 * kb + 512)
        picked_scales = keep.tile([P, S], U8, name="picked_scales", align_bytes=64)
        v_words = [placed("v_words0", [P, S], U32, 24 * kb), keep.tile([P, S], U32, name="v_words1", align_bytes=64)]
        v_scales = keep.tile([P, S], U8, name="v_scales", align_bytes=64)
        w1_first = placed("w1_first", [P, PASSES, PACK, P], F32, 100 * kb)
        w1_second = placed("w1_second", [P, PASSES, PACK, P], F32, 12 * kb)
        w1_pair = placed("w1_pair", [P, PASSES, PACK, 2 * P], F32, 4 * kb)
        w1_dealt = [
            placed("w1_dealt%d" % a, [P, PACK, BANK], F32, dealt_place + a * PACK * 4 * BANK) for a in range(PASSES)
        ]
        w1_raw = [w1_first[:], w1_second[:], w1_pair[:, :, :, 0:P], w1_pair[:, :, :, P : 2 * P]]
        w1_cast = [
            placed("w1_cast0", [P, 2, PASSES, BANK], BF16, 78 * kb),
            placed("w1_cast1", [P, 2, PASSES, BANK], BF16, 95 * kb),
            keep.tile([P, 2, PASSES, BANK], BF16, name="w1_cast2", align_bytes=64),
            placed("w1_cast3", [P, 2, PASSES, BANK], BF16, old_place[2]),
        ]
        cast_first = placed("cast_first", [P, PASSES, BANK], BF16, 4 * kb)
        w1_words = keep.tile([P, 2, PASSES * P], U32, name="w1_words", align_bytes=64)
        w1_scales = keep.tile([P, 2, PASSES * P], U8, name="w1_scales", align_bytes=64)
        first_parts = ((0, BANK // 2), (BANK // 2, BANK // 2), (BANK, BANK))
        first_place = (56 * kb - 512, 60 * kb - 512, 15 * kb)
        h_first = [placed("h_first%d" % i, [P, width], F32, first_place[i]) for i, (first, width) in enumerate(first_parts)]
        h_sb = [None] + [placed("h_sb%d" % s, [P, S], F32, h_place[s]) for s in range(1, SLICES)]
        wgs_plain = placed("wgs_plain", [P, S], F32, 0)
        wgs_dealt = [placed("wgs_dealt%d" % u, [P, 2, S], F32, (16 * kb, 88 * kb)[u]) for u in range(2)]
        old_sb = [placed("old_sb%d" % s, [P, T2], F32, old_place[s % OLD_BUFS]) for s in range(SLICES)]
        pages = tiles("page", 1, [P, T2], F32)
        pages.append(reuse.tile([P, T2], F32, name="page1", align_bytes=64, offset=28 * kb))
        z_turned = tiles("z_turned", CHUNKS, [P, 4, 2, 2 * P], BF16)
        z_low = tiles("z_low", CHUNKS - 1, [P, 4, 2 * P], BF16)
        z_low.append(placed("z_low_last", [P, 4, 2 * P], BF16, low_place))
        woven_first = keep.tile([P, CHUNKS, BANK * PACK], BF16, name="woven_first", align_bytes=64)
        woven_second = [
            placed("woven_second%d" % c, [P, BANK * PACK], BF16, dealt_place + c * 2 * BANK * PACK) for c in range(CHUNKS)
        ]
        early_words = placed("early_words", [P, 2, BANK], U32, 44 * kb)
        early_scales = keep.tile([P, 2, BANK], U8, name="early_scales", align_bytes=64)
        late_words = [placed("late_words%d" % i, [P, BANK], U32, dealt_place + i * 4 * BANK) for i in range(2)]
        z_words = [early_words[:, 0], early_words[:, 1], late_words[0][:], late_words[1][:]]
        z_words.extend([t[:] for t in tiles("z_words", CHUNKS, [P, BANK], U32)])
        z_scales = [early_scales[:, 0], early_scales[:, 1]]
        z_scales.extend([t[:] for t in tiles("z_scales", CHUNKS + 2, [P, BANK], U8)])
        w2_sb = placed("w2_sb", [P, PASSES, 2 * N], U8, 98 * kb)
        w2_planes = placed("w2_planes", [P, PASSES, N], U8, 97 * kb)
        bo_rows = placed("bo_rows", [P, P], F32, 96 * kb)
        ident = keep.tile([P, P], F32, name="ident")
        bias_rows = keep.tile([P, P], F32, name="bias_rows")
        bias = keep.tile([P, PACK], F32, name="bias")
        bias_out = keep.tile([P, N_TILES], F32, name="bias_out")
        bias_dealt = placed("bias_dealt", [P, PACK], F32, 100 * kb)

        def load_w1(raw, first, width):
            for a in range(PASSES):
                rows = w1[a * BANK : (a + 1) * BANK, first : first + width]
                nc.sync.dma_start(out=raw[:, a], in_=rows.rearrange("(p j) c -> p j c", j=PACK))

        def load_table(a):
            nc.sync.dma_start(
                out=table[a][:].bitcast(I32), in_=tab_words[a].rearrange("p t i -> p (t i)").bitcast(I32)
            )

        def load_old(s):
            if s < PACK:
                rows = old[s * P : (s + 1) * P, :]
            else:
                rows = old[BANK:H, :].rearrange("(p t) c -> p t c", t=PACK)[:, s - PACK, :]
            nc.sync.dma_start(out=old_sb[s][:], in_=rows)

        def load_wgs_dealt(u):
            rows = wgs.rearrange("(m t) j -> m t j", t=PACK)[:, 2 * u : 2 * u + 2, :]
            for q in (0, 2, 1, 3):
                nc.sync.dma_start(out=wgs_dealt[u][32 * q : 32 * (q + 1)], in_=rows)

        def cast_w1(s):
            dst = cast_first[:] if s == 0 else w1_cast[s // 2][:, s % 2]
            nc.scalar.copy(
                out=dst.rearrange("p a (c j) -> p a c j", j=PACK),
                in_=w1_raw[s].rearrange("p a j c -> p a c j"),
            )

        def cast_w1_dealt(u):
            for a in range(PASSES):
                nc.scalar.copy(
                    out=w1_cast[2 + u][:, :, a, :].rearrange("p e (m j) -> p m e j", j=PACK),
                    in_=w1_dealt[a][:].rearrange("p j (m t) -> p m t j", t=PACK)[:, :, 2 * u : 2 * u + 2, :],
                )

        def quantize_w1(s, count):
            part = slice(s % 2, s % 2 + count)
            src = cast_first[:].rearrange("p a w -> p (a w)") if s == 0 else None
            nc.vector.quantize_mx(
                out=w1_words[:, part].rearrange("p s w -> p (s w)").bitcast(FP8X4),
                scales=w1_scales[:, part].rearrange("p s w -> p (s w)"),
                in_=src if s == 0 else w1_cast[s // 2][:, part].rearrange("p s a w -> p (s a w)"),
            )

        def entries(lst, first, width):
            return lst[:, first // 16 : (first + width) // 16]

        def first_product(s, bank, first, width):
            entry_cols = slice(first, first + width)
            for a in range(PASSES):
                cols = slice(a * P, (a + 1) * P)
                nc.tensor.matmul_mx(
                    out=bank[:, 0:width],
                    lhsT=w1_words[:, s % 2, cols].bitcast(FP8X4),
                    lhsT_scale=w1_scales[:, s % 2, cols],
                    rhs=v_words[a][:, entry_cols].bitcast(FP8X4),
                    rhs_scale=v_scales[4 * a : P, entry_cols],
                    start=(a == 0),
                    stop=(a == PASSES - 1),
                )

        def relu(s, dst, src):
            col = bias[:, s : s + 1] if s < PACK else bias_dealt[:, s - PACK : s - PACK + 1]
            nc.scalar.activation(out=dst, in_=src, func=ACT.Relu, bias=col)

        def first_layer(s):
            for half in range(HALVES):
                bank = h_banks(s)[half]
                first_product(s, bank, half * BANK, BANK)
                relu(s, h_sb[s][:, half * BANK : (half + 1) * BANK], bank[:])

        def scatter(s):
            weight = wgs_plain[:] if s < PACK else wgs_dealt[(s - PACK) // 2][:, s % 2, :]
            nc.vector.tensor_tensor(pages[s % PAGE_BUFS][:].indirect(list2[:]), h_sb[s][:], weight, ALU.mult)

        def scatter_first(i):
            first, width = first_parts[i]
            nc.vector.tensor_tensor(
                pages[0][:].indirect(entries(list2, first, width)),
                h_first[i][:],
                wgs_plain[:, first : first + width],
                ALU.mult,
            )

        def turn(s, src, c, start, stop):
            for q in range(4):
                cols = slice(c * BANK + q * P, c * BANK + (q + 1) * P)
                nc.tensor.matmul(
                    sum_banks(s)[c][:, q * P : (q + 1) * P],
                    lhsT=src[:, cols],
                    rhs=ident[:],
                    is_transpose=True,
                    start=(start and q == 0),
                    stop=(stop and q == 3),
                )

        def pair_words(a, c, u):
            return z_low[c][:] if (a, u) == (1, 0) else z_turned[c][:, :, u, :]

        def round_sum(s, c):
            bank = sum_banks(s)[c]
            if s < PACK:
                nc.scalar.copy(
                    out=z_turned[c][:, :, :, s * 64 : (s + 1) * 64].rearrange("p q u (m e) -> p u q m e", e=2),
                    in_=bank[:].rearrange("p (q m u e) -> p u q m e", q=4, u=2, e=2),
                )
            else:
                u, e = divmod(s - PACK, 2)
                nc.scalar.copy(
                    out=pair_words(1, c, u).rearrange("p q (m e) -> p q m e", e=2)[:, :, :, e],
                    in_=bank[:].rearrange("p (q m) -> p q m", q=4),
                )

        def turn_back(a, c):
            pair = word_banks if a == 0 else out_banks[2 * c : 2 * c + 2]
            woven = (woven_first[:, c] if a == 0 else woven_second[c][:]).bitcast(F32)
            for b in range(2):
                for i in range(4):
                    q, u = 2 * b + i // 2, i % 2
                    nc.tensor.transpose(
                        pair[b][:, i * P : (i + 1) * P], pair_words(a, c, u)[:, q, :].bitcast(F32), ident[:]
                    )
                nc.scalar.copy(
                    out=woven[:, b * BANK : (b + 1) * BANK].rearrange("p (q t u) -> p q t u", q=2, u=2),
                    in_=pair[b][:].rearrange("p (q u t) -> p q t u", q=2, u=2),
                )

        def second_product(c, n, a):
            nc.tensor.matmul_mx(
                out=out_banks[(c * N_TILES + n) % len(out_banks)][:],
                lhsT=w2_sb[:, a, 2 * n * P : 2 * (n + 1) * P].bitcast(FP4X4),
                lhsT_scale=w2_planes[:, a, n * P : (n + 1) * P],
                rhs=z_words[a * CHUNKS + c].bitcast(FP8X4),
                rhs_scale=z_scales[a * CHUNKS + c],
                start=(a == 0),
                stop=(a == PASSES - 1),
            )

        def move_scales(a, q):
            first = SCALE_ROWS_AT + 16 * a + 4 * q
            nc.sync.dma_start(
                out=v_scales[32 * q + 4 * a : 32 * q + 4 * a + 4, :].bitcast(I32),
                in_=picked_scales[first : first + 4, :].bitcast(I32),
            )

        nc.gpsimd.memset(bias_rows[:], 0.0)
        nc.vector.memset(table_scales[0:SCALE_ROWS_AT, :].bitcast(I32), 0)
        nc.vector.memset(v_scales[:].bitcast(I32), 0)
        make_identity(nc, ident[:])
        nc.vector.memset(pages[0][:], 0.0)

        nc.sync.dma_start(list1[:], offs)
        nc.sync.dma_start(
            out=table_scales[SCALE_ROWS_AT:P, :].bitcast(I32), in_=tab_scales.rearrange("a r t -> (a r) t").bitcast(I32)
        )
        load_table(0)
        nc.sync.dma_start(out=bias_rows[0:PACK, :], in_=b1[0:BANK].rearrange("(s p) -> s p", p=P))
        load_w1(w1_first, 0, P)
        nc.sync.dma_start(list2[:], offs2)
        nc.vector.tensor_copy(picked_scales[:], table_scales[:].indirect(list1[:]))
        nc.vector.memset(pages[1][:], 0.0)
        moves = [(a, q) for a in range(PASSES) for q in range(4)]
        for a, q in moves[:2]:
            move_scales(a, q)
        load_table(1)
        for a, q in moves[2:]:
            move_scales(a, q)

        nc.tensor.transpose(word_banks[0][:, 0:P], bias_rows[:], ident[:])
        nc.scalar.activation(out=bias[:], in_=word_banks[0][:, 0:PACK], func=ACT.Identity)

        nc.vector.tensor_copy(v_words[0][:], table[0][:].indirect(list1[:]))
        nc.sync.dma_start(out=wgs_plain[:, 0:BANK], in_=wgs[:, 0:BANK])
        load_w1(w1_second, P, P)
        nc.sync.dma_start(out=wgs_plain[:, BANK:S], in_=wgs[:, BANK:S])
        cast_w1(0)
        quantize_w1(0, 1)
        load_w1(w1_pair, 2 * P, 2 * P)
        for first, width in first_parts:
            nc.vector.tensor_copy(
                v_words[1][:, first : first + width], table[1][:].indirect(entries(list1, first, width))
            )
        for a in range(PASSES):
            rows = w1[a * BANK : (a + 1) * BANK, BANK:H]
            nc.sync.dma_start(out=w1_dealt[a][:], in_=rows.rearrange("(p j) c -> p j c", j=PACK))
        for i, bank in enumerate(h_banks(0) + [word_banks[1]]):
            first, width = first_parts[i]
            first_product(0, bank, first, width)
            if i == 2:
                cast_w1(1)
            relu(0, h_first[i][:], bank[:, 0:width])
        scatter_first(0)
        scatter_first(1)
        quantize_w1(1, 1)
        cast_w1(2)
        cast_w1(3)
        first_layer(1)
        scatter_first(2)
        quantize_w1(2, 2)
        nc.sync.dma_start(out=bias_dealt[:], in_=b1[BANK:H].rearrange("(p t) -> p t", t=PACK))
        load_old(0)
        load_old(1)
        load_old(2)
        load_old(3)
        load_wgs_dealt(0)
        load_wgs_dealt(1)
        nc.sync.dma_start(out=w2_sb[:].bitcast(I32), in_=w2_words.rearrange("a p c -> p a c").bitcast(I32))
        nc.gpsimd.memset(w2_planes[:].rearrange("p a c -> p (a c)").bitcast(I32), 0)
        for q in range(4):
            nc.sync.dma_start(
                out=w2_planes[32 * q : 32 * q + 4].bitcast(I32),
                in_=w2_scales[:, 4 * q : 4 * q + 4, :].rearrange("a r c -> r a c").bitcast(I32),
            )

        staged = [
            placed("staged%d" % c, [P, N_TILES, BANK], F32, (old_place[0], old_place[1], old_place[2], 0)[c])
            for c in range(CHUNKS)
        ]
        outputs = [(c, n) for c in range(CHUNKS) for n in range(N_TILES)]
        held = outputs[0:8]

        for s in range(LAST):
            if s > 0:
                scatter(s)
            if s in (2, 4):
                quantize_w1(s + 2, 2)
            if s + 2 < SLICES:
                first_layer(s + 2)
            if s == 0:
                cast_w1_dealt(0)
            for c in range(CHUNKS):
                turn(s, pages[s % PAGE_BUFS], c, s == 0, s > 0)
                if s == 0:
                    continue
                round_sum(s, c)
            if s == 0:
                for c in range(CHUNKS):
                    turn(s, old_sb[s], c, False, True)
                    round_sum(s, c)
            if s + 1 < LAST:
                for c in (2, 3, 0, 1):
                    turn(s + 1, old_sb[s + 1], c, True, False)
            if s == 1:
                cast_w1_dealt(1)
                nc.gpsimd.memset(bo_rows[:], 0.0)
                nc.sync.dma_start(out=bo_rows[0:N_TILES, :], in_=bo.rearrange("(s p) -> s p", p=P))
                nc.tensor.transpose(word_banks[0][:, 0:P], bo_rows[:], ident[:])
                nc.scalar.activation(out=bias_out[:], in_=word_banks[0][:, 0:N_TILES], func=ACT.Identity)
            for later in {0: (4, 5), 2: (7,), 4: (6,)}.get(s, ()):
                load_old(later)
            for c in {3: (0, 1), 4: (2,), 5: (3,)}.get(s, ()):
                turn_back(0, c)
            if s == 5:
                nc.vector.quantize_mx(
                    out=early_words[:].rearrange("p c w -> p (c w)").bitcast(FP8X4),
                    scales=early_scales[:].rearrange("p c w -> p (c w)"),
                    in_=woven_first[:, 0:2].rearrange("p c w -> p (c w)"),
                )

        for c in range(CHUNKS):
            turn_back(1, c)
        for c, n in held:
            second_product(c, n, 0)
        scatter(LAST)
        for i, (first, width) in enumerate(((0, 256), (256, 256), (512, 512), (1024, 512), (1536, 256), (1792, 256))):
            z_last = placed("z_last%d" % i, [P, width], BF16, low_place + (i % 2) * 2 * BANK)
            c, start = divmod(first, BANK)
            cols = slice(first, first + width)
            part = slice(start, start + width)
            nc.vector.tensor_tensor(
                z_last[:], pages[LAST % PAGE_BUFS][:, cols], old_sb[LAST][:, cols], ALU.add
            )
            nc.vector.tensor_copy(
                out=woven_second[c][:].rearrange("p (w t) -> p w t", t=PACK)[:, part, PACK - 1], in_=z_last[:]
            )
            nc.vector.quantize_mx(
                out=z_words[CHUNKS + c][:, part].bitcast(FP8X4),
                scales=z_scales[CHUNKS + c][:, part],
                in_=woven_second[c][:, PACK * start : PACK * (start + width)],
            )
            if c in (1, 2):
                nc.vector.quantize_mx(
                    out=z_words[c + 1].bitcast(FP8X4), scales=z_scales[c + 1], in_=woven_first[:, c + 1]
                )
        for c, n in outputs[:-N_TILES]:
            if (c, n) not in held:
                second_product(c, n, 0)
            second_product(c, n, 1)
            bank = out_banks[(c * N_TILES + n) % len(out_banks)]
            dst = staged[c][:, n, :]
            col = bias_out[:, n : n + 1]
            nc.scalar.activation(out=dst, in_=bank[:], func=ACT.Identity, bias=col)
            cols = slice(c * BANK, (c + 1) * BANK)
            if (c, n) in outputs[0:2]:
                nc.sync.dma_start(out=out[n * P : (n + 1) * P, cols], in_=dst)
            elif n % 2 == 1:
                nc.sync.dma_start(
                    out=out[(n - 1) * P : (n + 1) * P, cols].rearrange("(n p) c -> p n c", p=P),
                    in_=staged[c][:, n - 1 : n + 1, :],
                )
        c = CHUNKS - 1
        for half in range(2):
            for pair in range(2):
                bank = out_banks[N_TILES + 2 * half + pair]
                for a in range(PASSES):
                    for i in range(2):
                        n = 2 * pair + i
                        part = slice(half * 2 * P, (half + 1) * 2 * P)
                        nc.tensor.matmul_mx(
                            out=bank[:, i * 2 * P : (i + 1) * 2 * P],
                            lhsT=w2_sb[:, a, 2 * n * P : 2 * (n + 1) * P].bitcast(FP4X4),
                            lhsT_scale=w2_planes[:, a, n * P : (n + 1) * P],
                            rhs=z_words[a * CHUNKS + c][:, part].bitcast(FP8X4),
                            rhs_scale=z_scales[a * CHUNKS + c][:, part],
                            start=(a == 0 and i == 0),
                            stop=(a == PASSES - 1 and i == 1),
                        )
                part = slice(half * 2 * P, (half + 1) * 2 * P)
                cols = slice(c * BANK + half * 2 * P, c * BANK + (half + 1) * 2 * P)
                for i in range(2):
                    n = 2 * pair + i
                    dst = staged[c][:, n, part]
                    src = bank[:, i * 2 * P : (i + 1) * 2 * P]
                    if pair == 1:
                        nc.vector.tensor_scalar_add(dst, src, bias_out[:, n : n + 1])
                    else:
                        nc.scalar.activation(out=dst, in_=src, func=ACT.Identity, bias=bias_out[:, n : n + 1])
                    if half == 1:
                        nc.sync.dma_start(out=out[n * P : (n + 1) * P, cols], in_=dst)
                if half == 0:
                    nc.sync.dma_start(
                        out=out[2 * pair * P : 2 * (pair + 1) * P, cols].rearrange("(n p) c -> p n c", p=P),
                        in_=staged[c][:, 2 * pair : 2 * pair + 2, part],
                    )
